import numpy as np
import ml_dtypes


def mxq(x, axis, fmt="e4m3"):
    dtype, down = {"e4m3": (ml_dtypes.float8_e4m3fn, 7), "e5m2": (ml_dtypes.float8_e5m2, 14)}[fmt]
    v = np.moveaxis(np.asarray(x, np.float32).astype(ml_dtypes.bfloat16).astype(np.float64), axis, -1)
    blocks = v.reshape(v.shape[:-1] + (-1, 32))
    amax = np.abs(blocks).max(-1, keepdims=True)
    byte = np.maximum(np.where(amax > 0, np.frexp(amax)[1] - 1 + 127, 0) - down, 1)
    scale = np.exp2(byte - 127.0)
    codes = (blocks / scale).astype(np.float32).astype(dtype).astype(np.float64)
    return np.moveaxis((codes * scale).reshape(v.shape), -1, axis)


WIDE = False


def mx_kscale(k):
    if not WIDE:
        return np.ones(k)
    levels = np.array([10, -10, 5, -5, 0])
    if k % 512:
        return np.exp2(np.random.permutation(np.resize(levels, k // 32))).repeat(32)
    a = np.empty((k // 512, 16))
    for p in range(k // 512):
        a[p, :8] = np.random.permutation(np.resize(levels, 8))
        for g in range(8):
            far = levels[np.abs(levels - a[p, g]) >= 10]
            a[p, g + 8] = far[np.random.randint(len(far))]
    return np.exp2(a.ravel()).repeat(32)


def f64(x):
    return np.asarray(x).astype(np.float64)


def striped(idx):
    return np.tile(idx.reshape(-1, 16).T, (8, 1)).astype(np.uint16)


def unstriped(offs):
    return offs[:16].T.reshape(-1).astype(np.int64)


def pack_weight(w):
    k, n = w.shape
    w = f64(np.asarray(w, np.float32).astype(ml_dtypes.bfloat16)).reshape(k // 32, 32, n)
    amax = np.abs(w).max(1)
    byte = np.clip(np.where(amax > 0, np.frexp(amax)[1] - 1 + 127 - 7, 1), 1, 254)
    scaled = (w * np.exp2(127.0 - byte)[:, None, :]).reshape(k, n).astype(np.float32)
    words = np.ascontiguousarray(scaled.reshape(k // 512, 128, 4, n).transpose(0, 1, 3, 2)).astype(ml_dtypes.float8_e4m3fn).view(np.uint8)
    return words, np.ascontiguousarray(byte.astype(np.uint8).reshape(k // 512, 16, n))


def unpack_weight(words, scales):
    g, p, n, _ = words.shape
    vals = np.ascontiguousarray(words).view(ml_dtypes.float8_e4m3fn).astype(np.float64) * np.repeat(np.exp2(scales.astype(np.float64) - 127.0), 8, axis=1)[..., None]
    return vals.transpose(0, 1, 3, 2).reshape(g * 512, n)


K, T, S, H, N = 512, 2048, 1024, 512, 256


def setup_inputs():
    n = np.random.standard_normal
    s = mx_kscale(K)[:, None]
    u = mx_kscale(H)
    packed_xT = pack_weight(n((K, T)) * s)
    packed_w2 = pack_weight(n((H, N)) / np.sqrt(H) / u[:, None])
    return {
        "x_words": packed_xT[0],
        "x_scales": packed_xT[1],
        "w1": (n((K, H)) / np.sqrt(K) / s * u).astype(np.float32),
        "w2_words": packed_w2[0],
        "w2_scales": packed_w2[1],
        "pos": (0.5 * n((H, S)) * u[:, None]).astype(np.float32),
        "offs": striped(np.random.permutation(T)[(T * np.random.uniform(0, 1, S) ** 4).astype(np.int64)]),
    }


def reference(x_words, x_scales, w1, w2_words, w2_scales, pos, offs):
    xq = unpack_weight(x_words, x_scales)[:, unstriped(offs)]
    h = (mxq(f64(w1), 0, "e4m3").T @ xq) + f64(pos)
    return unpack_weight(w2_words, w2_scales).T @ mxq(h, 0, "e4m3")

@@ -1,0 +1,147 @@
+from contextlib import ExitStack
+
+import concourse.mybir as mybir
+
+K, T, S, H, N = 512, 2048, 1024, 512, 256
+FLOPS = 2 * K * H * S + 2 * H * N * S
+
+F32 = mybir.dt.float32
+BF16 = mybir.dt.bfloat16
+I32 = mybir.dt.int32
+U32 = mybir.dt.uint32
+U16 = mybir.dt.uint16
+U8 = mybir.dt.uint8
+FP8X4 = mybir.dt.float8_e4m3fn_x4
+ADD = mybir.AluOpType.add
+
+P = 128
+PACK = 4
+CHUNK = 128
+GATHER = 512
+POS_LOAD = 256
+GROUPS = (256, 256, 256, 128, 128)
+
+
+def load_scale_rows(nc, plane, rows):
+    for q in range(4):
+        nc.sync.dma_start(out=plane[32 * q : 32 * q + 4, :].bitcast(I32), in_=rows[4 * q : 4 * q + 4, :].bitcast(I32))
+
+
+def tile_picked_embpos_none_p_kernel(tc, x_words, x_scales, w1, w2_words, w2_scales, pos, offs, out):
+    nc = tc.nc
+    with ExitStack() as ctx:
+        keep = ctx.enter_context(tc.tile_pool(name="keep", bufs=1))
+        hid_psum = ctx.enter_context(tc.psum_pool(name="hid_psum", bufs=5))
+        out_psum = ctx.enter_context(tc.psum_pool(name="out_psum", bufs=3))
+
+        offsets = keep.tile([P, S // 16], U16, name="offsets")
+        table_words = keep.tile([P, T], I32, name="table_words", align_bytes=64)
+        table_scales = keep.tile([P, T], U8, name="table_scales", align_bytes=64)
+        w2_codes = keep.tile([P, N], I32, name="w2_codes", align_bytes=64)
+        w2_plane = keep.tile([P, N], U8, name="w2_plane", align_bytes=64)
+
+        nc.vector.memset(table_scales[:].bitcast(I32), 0)
+        nc.vector.memset(w2_plane[:].bitcast(I32), 0)
+
+        nc.sync.dma_start(offsets[:], offs)
+        load_scale_rows(nc, table_scales, x_scales[0])
+        nc.sync.dma_start(out=table_words[:], in_=x_words[0].rearrange("p c r -> p (c r)").bitcast(I32))
+        w1_rows = w1.rearrange("(p j) c -> p j c", j=PACK)
+        w1_raw = []
+        for half in range(2):
+            raw = keep.tile([P, PACK, H // 2], F32, name=f"w1_raw{half}")
+            nc.sync.dma_start(out=raw[:], in_=w1_rows[:, :, half * (H // 2) : (half + 1) * (H // 2)])
+            w1_raw.append(raw)
+        pos_rows = pos.rearrange("(p t) s -> p t s", t=PACK)
+        pos_sb = []
+        for g in range(S // POS_LOAD):
+            part = keep.tile([P, PACK, POS_LOAD], F32, name=f"pos{g}")
+            nc.sync.dma_start(out=part[:], in_=pos_rows[:, :, g * POS_LOAD : (g + 1) * POS_LOAD])
+            pos_sb.append(part)
+            if g == 0:
+                nc.sync.dma_start(out=w2_codes[:], in_=w2_words[0].rearrange("p c r -> p (c r)").bitcast(I32))
+                load_scale_rows(nc, w2_plane, w2_scales[0])
+
+        x_codes, x_plane = [], []
+        for g in range(S // GATHER):
+            plane = keep.tile([P, GATHER], U8, name=f"x_plane{g}", align_bytes=64)
+            cols = slice(g * GATHER // 16, (g + 1) * GATHER // 16)
+            nc.vector.tensor_copy(out=plane[:], in_=table_scales[:].indirect(offsets[:, cols]))
+            x_plane.append(plane)
+        for g in range(S // GATHER):
+            codes = keep.tile([P, GATHER], U32, name=f"x_codes{g}", align_bytes=64)
+            cols = slice(g * GATHER // 16, (g + 1) * GATHER // 16)
+            nc.vector.tensor_copy(out=codes[:], in_=table_words[:].bitcast(U32).indirect(offsets[:, cols]))
+            x_codes.append(codes)
+
+        w1_grouped = keep.tile([P, PACK, P, PACK], BF16, name="w1_grouped", align_bytes=64)
+        for half in range(2):
+            nc.scalar.copy(
+                out=w1_grouped[:, :, half * (P // 2) : (half + 1) * (P // 2), :].rearrange("p t m j -> p m j t"),
+                in_=w1_raw[half][:].rearrange("p j (m t) -> p m j t", t=PACK),
+            )
+        w1_codes = keep.tile([P, H], U32, name="w1_codes", align_bytes=64)
+        w1_plane = keep.tile([P, H], U8, name="w1_plane", align_bytes=64)
+        nc.vector.quantize_mx(
+            out=w1_codes[:].bitcast(FP8X4),
+            scales=w1_plane[:],
+            in_=w1_grouped[:].rearrange("p t m j -> p (t m j)"),
+        )
+
+        out_rows = out.rearrange("(a p) s -> p a s", p=P)
+
+        def hidden(s0, h_bf, lo):
+            bank = hid_psum.tile([P, PACK, CHUNK], F32, name="hid_bank")
+            g, c0 = divmod(s0, GATHER)
+            for t in range(PACK):
+                nc.tensor.matmul_mx(
+                    out=bank[:, t, :],
+                    lhsT=w1_codes[:, t * P : (t + 1) * P].bitcast(FP8X4),
+                    lhsT_scale=w1_plane[:, t * P : (t + 1) * P],
+                    rhs=x_codes[g][:, c0 : c0 + CHUNK].bitcast(FP8X4),
+                    rhs_scale=x_plane[g][:, c0 : c0 + CHUNK],
+                    start=True,
+                    stop=True,
+                )
+            pg, p0 = divmod(s0, POS_LOAD)
+            nc.vector.tensor_tensor(
+                out=h_bf[:, lo : lo + CHUNK, :].rearrange("p (c i) t -> p c t i", i=2),
+                in0=bank[:].rearrange("p t (c i) -> p c t i", i=2),
+                in1=pos_sb[pg][:, :, p0 : p0 + CHUNK].rearrange("p t (c i) -> p c t i", i=2),
+                op=ADD,
+            )
+
+        def second(s0, width, h_bf, gi):
+            h_codes = keep.tile([P, width], U32, name=f"h_codes{gi}", align_bytes=64)
+            h_plane = keep.tile([P, width], U8, name=f"h_plane{gi}", align_bytes=64)
+            nc.vector.quantize_mx(
+                out=h_codes[:].bitcast(FP8X4),
+                scales=h_plane[:],
+                in_=h_bf[:].rearrange("p s t -> p (s t)"),
+            )
+            bank = out_psum.tile([P, N // P, width], F32, name="out_bank")
+            for a in range(N // P):
+                nc.tensor.matmul_mx(
+                    out=bank[:, a, :],
+                    lhsT=w2_codes[:, a * P : (a + 1) * P].bitcast(FP8X4),
+                    lhsT_scale=w2_plane[:, a * P : (a + 1) * P],
+                    rhs=h_codes[:].bitcast(FP8X4),
+                    rhs_scale=h_plane[:],
+                    start=True,
+                    stop=True,
+                )
+            result = keep.tile([P, N // P, width], F32, name=f"result{gi}")
+            nc.scalar.copy(out=result[:], in_=bank[:])
+            nc.sync.dma_start(out=out_rows[:, :, s0 : s0 + width], in_=result[:])
+
+        s0 = 0
+        waiting = None
+        for gi, width in enumerate(GROUPS):
+            h_bf = keep.tile([P, width, PACK], BF16, name=f"h_bf{gi}", align_bytes=64)
+            for lo in range(0, width, CHUNK):
+                hidden(s0 + lo, h_bf, lo)
+                if lo == 0 and waiting is not None:
+                    second(*waiting)
+            waiting = (s0, width, h_bf, gi)
+            s0 += width
+        second(*waiting)

@@ -22,45 +22,36 @@ POS_LOAD = 256
 GROUPS = (256, 256, 256, 128, 128)
 
 
-def load_scale_rows(nc, plane, rows):
+def load_scale_rows(queue, plane, rows):
     for q in range(4):
-        nc.sync.dma_start(out=plane[32 * q : 32 * q + 4, :].bitcast(I32), in_=rows[4 * q : 4 * q + 4, :].bitcast(I32))
+        queue.dma_start(out=plane[32 * q : 32 * q + 4, :].bitcast(I32), in_=rows[4 * q : 4 * q + 4, :].bitcast(I32))
 
 
 def tile_picked_embpos_none_p_kernel(tc, x_words, x_scales, w1, w2_words, w2_scales, pos, offs, out):
     nc = tc.nc
     with ExitStack() as ctx:
         keep = ctx.enter_context(tc.tile_pool(name="keep", bufs=1))
-        hid_psum = ctx.enter_context(tc.psum_pool(name="hid_psum", bufs=5))
-        out_psum = ctx.enter_context(tc.psum_pool(name="out_psum", bufs=3))
+        hid_psum = ctx.enter_context(tc.psum_pool(name="hid_psum", bufs=4))
+        out_psum = ctx.enter_context(tc.psum_pool(name="out_psum", bufs=4))
 
         offsets = keep.tile([P, S // 16], U16, name="offsets")
-        table_words = keep.tile([P, T], I32, name="table_words", align_bytes=64)
-        table_scales = keep.tile([P, T], U8, name="table_scales", align_bytes=64)
-        w2_codes = keep.tile([P, N], I32, name="w2_codes", align_bytes=64)
-        w2_plane = keep.tile([P, N], U8, name="w2_plane", align_bytes=64)
-
-        nc.vector.memset(table_scales[:].bitcast(I32), 0)
-        nc.vector.memset(w2_plane[:].bitcast(I32), 0)
-
         nc.sync.dma_start(offsets[:], offs)
-        load_scale_rows(nc, table_scales, x_scales[0])
-        nc.sync.dma_start(out=table_words[:], in_=x_words[0].rearrange("p c r -> p (c r)").bitcast(I32))
+
+        table_scales = keep.tile([P, T], U8, name="table_scales", tag="scales", align_bytes=64)
+        nc.vector.memset(table_scales[:].bitcast(I32), 0)
+
         w1_rows = w1.rearrange("(p j) c -> p j c", j=PACK)
         w1_raw = []
         for half in range(2):
-            raw = keep.tile([P, PACK, H // 2], F32, name=f"w1_raw{half}")
+            raw = keep.tile([P, PACK, H // 2], F32, name=f"w1_raw{half}", tag=f"slot{half}", align_bytes=64)
             nc.sync.dma_start(out=raw[:], in_=w1_rows[:, :, half * (H // 2) : (half + 1) * (H // 2)])
             w1_raw.append(raw)
-        pos_rows = pos.rearrange("(p t) s -> p t s", t=PACK)
-        pos_sb = []
-        for g in range(S // POS_LOAD):
-            part = keep.tile([P, PACK, POS_LOAD], F32, name=f"pos{g}")
-            nc.sync.dma_start(out=part[:], in_=pos_rows[:, :, g * POS_LOAD : (g + 1) * POS_LOAD])
-            pos_sb.append(part)
-            if g == 0:
-                nc.sync.dma_start(out=w2_codes[:], in_=w2_words[0].rearrange("p c r -> p (c r)").bitcast(I32))
-                load_scale_rows(nc, w2_plane, w2_scales[0])
+            if half == 0:
+                load_scale_rows(nc.sync, table_scales, x_scales[0])
+        table_words = keep.tile([P, T], I32, name="table_words", tag="slot3", align_bytes=64)
+        nc.sync.dma_start(out=table_words[:], in_=x_words[0].rearrange("p c r -> p (c r)").bitcast(I32))
+        w2_codes = keep.tile([P, N], I32, name="w2_codes", align_bytes=64)
+        nc.sync.dma_start(out=w2_codes[:], in_=w2_words[0].rearrange("p c r -> p (c r)").bitcast(I32))
 
         x_codes, x_plane = [], []
         for g in range(S // GATHER):
@@ -68,13 +59,8 @@ def tile_picked_embpos_none_p_kernel(tc, x_words, x_scales, w1, w2_words, w2_sca
             cols = slice(g * GATHER // 16, (g + 1) * GATHER // 16)
             nc.vector.tensor_copy(out=plane[:], in_=table_scales[:].indirect(offsets[:, cols]))
             x_plane.append(plane)
-        for g in range(S // GATHER):
-            codes = keep.tile([P, GATHER], U32, name=f"x_codes{g}", align_bytes=64)
-            cols = slice(g * GATHER // 16, (g + 1) * GATHER // 16)
-            nc.vector.tensor_copy(out=codes[:], in_=table_words[:].bitcast(U32).indirect(offsets[:, cols]))
-            x_codes.append(codes)
 
-        w1_grouped = keep.tile([P, PACK, P, PACK], BF16, name="w1_grouped", align_bytes=64)
+        w1_grouped = keep.tile([P, PACK, P, PACK], BF16, name="w1_grouped", tag="slot2", align_bytes=64)
         for half in range(2):
             nc.scalar.copy(
                 out=w1_grouped[:, :, half * (P // 2) : (half + 1) * (P // 2), :].rearrange("p t m j -> p m j t"),
@@ -87,6 +73,23 @@ def tile_picked_embpos_none_p_kernel(tc, x_words, x_scales, w1, w2_words, w2_sca
             scales=w1_plane[:],
             in_=w1_grouped[:].rearrange("p t m j -> p (t m j)"),
         )
+
+        for g in range(S // GATHER):
+            codes = keep.tile([P, GATHER], U32, name=f"x_codes{g}", align_bytes=64)
+            cols = slice(g * GATHER // 16, (g + 1) * GATHER // 16)
+            nc.vector.tensor_copy(out=codes[:], in_=table_words[:].bitcast(U32).indirect(offsets[:, cols]))
+            x_codes.append(codes)
+
+        w2_plane = keep.tile([P, N], U8, name="w2_plane", tag="scales", align_bytes=64)
+        nc.vector.memset(w2_plane[:].bitcast(I32), 0)
+        load_scale_rows(nc.sync, w2_plane, w2_scales[0])
+
+        pos_rows = pos.rearrange("(p t) s -> p t s", t=PACK)
+        pos_sb = []
+        for g in range(S // POS_LOAD):
+            part = keep.tile([P, PACK, POS_LOAD], F32, name=f"pos{g}", tag=f"slot{g}", align_bytes=64)
+            nc.sync.dma_start(out=part[:], in_=pos_rows[:, :, g * POS_LOAD : (g + 1) * POS_LOAD])
+            pos_sb.append(part)
 
         out_rows = out.rearrange("(a p) s -> p a s", p=P)
 

@@ -18,13 +18,13 @@ P = 128
 PACK = 4
 CHUNK = 128
 GATHER = 512
-POS_LOAD = 256
+POS_LOADS = (384, 384, 256)
 GROUPS = (256, 256, 256, 128, 128)
 
 
-def load_scale_rows(queue, plane, rows):
+def load_scale_rows(queues, plane, rows):
     for q in range(4):
-        queue.dma_start(out=plane[32 * q : 32 * q + 4, :].bitcast(I32), in_=rows[4 * q : 4 * q + 4, :].bitcast(I32))
+        queues[q % len(queues)].dma_start(out=plane[32 * q : 32 * q + 4, :].bitcast(I32), in_=rows[4 * q : 4 * q + 4, :].bitcast(I32))
 
 
 def tile_picked_embpos_none_p_kernel(tc, x_words, x_scales, w1, w2_words, w2_scales, pos, offs, out):
@@ -35,9 +35,8 @@ def tile_picked_embpos_none_p_kernel(tc, x_words, x_scales, w1, w2_words, w2_sca
         out_psum = ctx.enter_context(tc.psum_pool(name="out_psum", bufs=4))
 
         offsets = keep.tile([P, S // 16], U16, name="offsets")
-        nc.sync.dma_start(offsets[:], offs)
 
-        table_scales = keep.tile([P, T], U8, name="table_scales", tag="scales", align_bytes=64)
+        table_scales = keep.tile([P, T], U8, name="table_scales", align_bytes=64)
         nc.vector.memset(table_scales[:].bitcast(I32), 0)
 
         w1_rows = w1.rearrange("(p j) c -> p j c", j=PACK)
@@ -47,8 +46,9 @@ def tile_picked_embpos_none_p_kernel(tc, x_words, x_scales, w1, w2_words, w2_sca
             nc.sync.dma_start(out=raw[:], in_=w1_rows[:, :, half * (H // 2) : (half + 1) * (H // 2)])
             w1_raw.append(raw)
             if half == 0:
-                load_scale_rows(nc.sync, table_scales, x_scales[0])
-        table_words = keep.tile([P, T], I32, name="table_words", tag="slot3", align_bytes=64)
+                nc.sync.dma_start(offsets[:], offs)
+                load_scale_rows((nc.sync, nc.scalar), table_scales, x_scales[0])
+        table_words = keep.tile([P, T], I32, name="table_words", tag="slot2", align_bytes=64)
         nc.sync.dma_start(out=table_words[:], in_=x_words[0].rearrange("p c r -> p (c r)").bitcast(I32))
         w2_codes = keep.tile([P, N], I32, name="w2_codes", align_bytes=64)
         nc.sync.dma_start(out=w2_codes[:], in_=w2_words[0].rearrange("p c r -> p (c r)").bitcast(I32))
@@ -60,36 +60,43 @@ def tile_picked_embpos_none_p_kernel(tc, x_words, x_scales, w1, w2_words, w2_sca
             nc.vector.tensor_copy(out=plane[:], in_=table_scales[:].indirect(offsets[:, cols]))
             x_plane.append(plane)
 
-        w1_grouped = keep.tile([P, PACK, P, PACK], BF16, name="w1_grouped", tag="slot2", align_bytes=64)
-        for half in range(2):
-            nc.scalar.copy(
-                out=w1_grouped[:, :, half * (P // 2) : (half + 1) * (P // 2), :].rearrange("p t m j -> p m j t"),
-                in_=w1_raw[half][:].rearrange("p j (m t) -> p m j t", t=PACK),
-            )
         w1_codes = keep.tile([P, H], U32, name="w1_codes", align_bytes=64)
         w1_plane = keep.tile([P, H], U8, name="w1_plane", align_bytes=64)
-        nc.vector.quantize_mx(
-            out=w1_codes[:].bitcast(FP8X4),
-            scales=w1_plane[:],
-            in_=w1_grouped[:].rearrange("p t m j -> p (t m j)"),
-        )
+        w1_grouped = [
+            keep.tile([P, 2, P, PACK], BF16, name=f"w1_grouped{u}", tag=f"late{u}", align_bytes=64) for u in range(2)
+        ]
+        for half in range(2):
+            for u in range(2):
+                nc.scalar.copy(
+                    out=w1_grouped[u][:, :, half * (P // 2) : (half + 1) * (P // 2), :].rearrange("p t m j -> p m j t"),
+                    in_=w1_raw[half][:].rearrange("p j (m t) -> p m j t", t=PACK)[:, :, :, 2 * u : 2 * u + 2],
+                )
+        for u in range(2):
+            cols = slice(u * 2 * P, (u + 1) * 2 * P)
+            nc.vector.quantize_mx(
+                out=w1_codes[:, cols].bitcast(FP8X4),
+                scales=w1_plane[:, cols],
+                in_=w1_grouped[u][:].rearrange("p t m j -> p (t m j)"),
+            )
 
         for g in range(S // GATHER):
-            codes = keep.tile([P, GATHER], U32, name=f"x_codes{g}", align_bytes=64)
+            codes = keep.tile([P, GATHER], U32, name=f"x_codes{g}", tag="late0" if g == 0 else "codes1", align_bytes=64)
             cols = slice(g * GATHER // 16, (g + 1) * GATHER // 16)
             nc.vector.tensor_copy(out=codes[:], in_=table_words[:].bitcast(U32).indirect(offsets[:, cols]))
             x_codes.append(codes)
 
-        w2_plane = keep.tile([P, N], U8, name="w2_plane", tag="scales", align_bytes=64)
-        nc.vector.memset(w2_plane[:].bitcast(I32), 0)
-        load_scale_rows(nc.sync, w2_plane, w2_scales[0])
+        w2_plane = keep.tile([P, N], U8, name="w2_plane", tag="late1", align_bytes=64)
+        nc.gpsimd.memset(w2_plane[:].bitcast(I32), 0)
+        load_scale_rows((nc.scalar,), w2_plane, w2_scales[0])
 
         pos_rows = pos.rearrange("(p t) s -> p t s", t=PACK)
         pos_sb = []
-        for g in range(S // POS_LOAD):
-            part = keep.tile([P, PACK, POS_LOAD], F32, name=f"pos{g}", tag=f"slot{g}", align_bytes=64)
-            nc.sync.dma_start(out=part[:], in_=pos_rows[:, :, g * POS_LOAD : (g + 1) * POS_LOAD])
-            pos_sb.append(part)
+        first = 0
+        for g, width in enumerate(POS_LOADS):
+            part = keep.tile([P, PACK, width], F32, name=f"pos{g}", tag=f"slot{g}", align_bytes=64)
+            nc.sync.dma_start(out=part[:], in_=pos_rows[:, :, first : first + width])
+            pos_sb.extend(part[:, :, lo : lo + CHUNK] for lo in range(0, width, CHUNK))
+            first += width
 
         out_rows = out.rearrange("(a p) s -> p a s", p=P)
 
@@ -106,11 +113,10 @@ def tile_picked_embpos_none_p_kernel(tc, x_words, x_scales, w1, w2_words, w2_sca
                     start=True,
                     stop=True,
                 )
-            pg, p0 = divmod(s0, POS_LOAD)
             nc.vector.tensor_tensor(
-                out=h_bf[:, lo : lo + CHUNK, :].rearrange("p (c i) t -> p c t i", i=2),
-                in0=bank[:].rearrange("p t (c i) -> p c t i", i=2),
-                in1=pos_sb[pg][:, :, p0 : p0 + CHUNK].rearrange("p t (c i) -> p c t i", i=2),
+                out=h_bf[:, lo : lo + CHUNK, :].rearrange("p (c i) t -> p c t i", i=4),
+                in0=bank[:].rearrange("p t (c i) -> p c t i", i=4),
+                in1=pos_sb[s0 // CHUNK].rearrange("p t (c i) -> p c t i", i=4),
                 op=ADD,
             )
 
@@ -122,8 +128,12 @@ def tile_picked_embpos_none_p_kernel(tc, x_words, x_scales, w1, w2_words, w2_sca
                 scales=h_plane[:],
                 in_=h_bf[:].rearrange("p s t -> p (s t)"),
             )
+            last = s0 + width == S
+            result = keep.tile([P, N // P, width], F32, name=f"result{gi}")
             bank = out_psum.tile([P, N // P, width], F32, name="out_bank")
             for a in range(N // P):
+                if last and a == 1:
+                    bank = out_psum.tile([P, N // P, width], F32, name="out_bank")
                 nc.tensor.matmul_mx(
                     out=bank[:, a, :],
                     lhsT=w2_codes[:, a * P : (a + 1) * P].bitcast(FP8X4),
@@ -133,8 +143,12 @@ def tile_picked_embpos_none_p_kernel(tc, x_words, x_scales, w1, w2_words, w2_sca
                     start=True,
                     stop=True,
                 )
-            result = keep.tile([P, N // P, width], F32, name=f"result{gi}")
-            nc.scalar.copy(out=result[:], in_=bank[:])
+                if last and a == 0:
+                    nc.scalar.copy(out=result[:, a, :], in_=bank[:, a, :])
+                if last and a == 1:
+                    nc.vector.tensor_copy(out=result[:, a, :], in_=bank[:, a, :])
+            if not last:
+                nc.scalar.copy(out=result[:], in_=bank[:])
             nc.sync.dma_start(out=out_rows[:, :, s0 : s0 + width], in_=result[:])
 
         s0 = 0

@@ -18,8 +18,7 @@ P = 128
 PACK = 4
 CHUNK = 128
 GATHER = 512
-POS_LOADS = (384, 384, 256)
-GROUPS = (256, 256, 256, 128, 128)
+POS_LOADS = (256, 256, 256, 256)
 
 
 def load_scale_rows(queues, plane, rows):
@@ -42,16 +41,28 @@ def tile_picked_embpos_none_p_kernel(tc, x_words, x_scales, w1, w2_words, w2_sca
         w1_rows = w1.rearrange("(p j) c -> p j c", j=PACK)
         w1_raw = []
         for half in range(2):
-            raw = keep.tile([P, PACK, H // 2], F32, name=f"w1_raw{half}", tag=f"slot{half}", align_bytes=64)
+            raw = keep.tile([P, PACK, H // 2], F32, name=f"w1_raw{half}")
             nc.sync.dma_start(out=raw[:], in_=w1_rows[:, :, half * (H // 2) : (half + 1) * (H // 2)])
             w1_raw.append(raw)
             if half == 0:
                 nc.sync.dma_start(offsets[:], offs)
                 load_scale_rows((nc.sync, nc.scalar), table_scales, x_scales[0])
-        table_words = keep.tile([P, T], I32, name="table_words", tag="slot2", align_bytes=64)
+        table_words = keep.tile([P, T], I32, name="table_words", align_bytes=64)
         nc.sync.dma_start(out=table_words[:], in_=x_words[0].rearrange("p c r -> p (c r)").bitcast(I32))
         w2_codes = keep.tile([P, N], I32, name="w2_codes", align_bytes=64)
-        nc.sync.dma_start(out=w2_codes[:], in_=w2_words[0].rearrange("p c r -> p (c r)").bitcast(I32))
+        w2_plane = keep.tile([P, N], U8, name="w2_plane", align_bytes=64)
+        nc.gpsimd.memset(w2_plane[:].bitcast(I32), 0)
+        pos_rows = pos.rearrange("(p t) s -> p t s", t=PACK)
+        pos_sb = []
+        first = 0
+        for g, width in enumerate(POS_LOADS):
+            part = keep.tile([P, PACK, width], F32, name=f"pos{g}")
+            nc.sync.dma_start(out=part[:], in_=pos_rows[:, :, first : first + width])
+            pos_sb.extend(part[:, :, lo : lo + CHUNK] for lo in range(0, width, CHUNK))
+            first += width
+            if g == 1:
+                nc.sync.dma_start(out=w2_codes[:], in_=w2_words[0].rearrange("p c r -> p (c r)").bitcast(I32))
+                load_scale_rows((nc.sync,), w2_plane, w2_scales[0])
 
         x_codes, x_plane = [], []
         for g in range(S // GATHER):
@@ -85,18 +96,6 @@ def tile_picked_embpos_none_p_kernel(tc, x_words, x_scales, w1, w2_words, w2_sca
             nc.vector.tensor_copy(out=codes[:], in_=table_words[:].bitcast(U32).indirect(offsets[:, cols]))
             x_codes.append(codes)
 
-        w2_plane = keep.tile([P, N], U8, name="w2_plane", tag="late1", align_bytes=64)
-        nc.gpsimd.memset(w2_plane[:].bitcast(I32), 0)
-        load_scale_rows((nc.scalar,), w2_plane, w2_scales[0])
-
-        pos_rows = pos.rearrange("(p t) s -> p t s", t=PACK)
-        pos_sb = []
-        first = 0
-        for g, width in enumerate(POS_LOADS):
-            part = keep.tile([P, PACK, width], F32, name=f"pos{g}", tag=f"slot{g}", align_bytes=64)
-            nc.sync.dma_start(out=part[:], in_=pos_rows[:, :, first : first + width])
-            pos_sb.extend(part[:, :, lo : lo + CHUNK] for lo in range(0, width, CHUNK))
-            first += width
 
         out_rows = out.rearrange("(a p) s -> p a s", p=P)
 
@@ -114,51 +113,60 @@ def tile_picked_embpos_none_p_kernel(tc, x_words, x_scales, w1, w2_words, w2_sca
                     stop=True,
                 )
             nc.vector.tensor_tensor(
-                out=h_bf[:, lo : lo + CHUNK, :].rearrange("p (c i) t -> p c t i", i=4),
-                in0=bank[:].rearrange("p t (c i) -> p c t i", i=4),
-                in1=pos_sb[s0 // CHUNK].rearrange("p t (c i) -> p c t i", i=4),
+                out=h_bf[:, lo : lo + CHUNK, :].rearrange("p (c i) t -> p c t i", i=2),
+                in0=bank[:].rearrange("p t (c i) -> p c t i", i=2),
+                in1=pos_sb[s0 // CHUNK].rearrange("p t (c i) -> p c t i", i=2),
                 op=ADD,
             )
 
-        def second(s0, width, h_bf, gi):
-            h_codes = keep.tile([P, width], U32, name=f"h_codes{gi}", align_bytes=64)
-            h_plane = keep.tile([P, width], U8, name=f"h_plane{gi}", align_bytes=64)
+        def quantize_hidden(h_bf, c):
+            h_codes = keep.tile([P, CHUNK], U32, name=f"h_codes{c}", align_bytes=64)
+            h_plane = keep.tile([P, CHUNK], U8, name=f"h_plane{c}", align_bytes=64)
             nc.vector.quantize_mx(
                 out=h_codes[:].bitcast(FP8X4),
                 scales=h_plane[:],
                 in_=h_bf[:].rearrange("p s t -> p (s t)"),
             )
-            last = s0 + width == S
-            result = keep.tile([P, N // P, width], F32, name=f"result{gi}")
-            bank = out_psum.tile([P, N // P, width], F32, name="out_bank")
-            for a in range(N // P):
-                if last and a == 1:
-                    bank = out_psum.tile([P, N // P, width], F32, name="out_bank")
-                nc.tensor.matmul_mx(
-                    out=bank[:, a, :],
-                    lhsT=w2_codes[:, a * P : (a + 1) * P].bitcast(FP8X4),
-                    lhsT_scale=w2_plane[:, a * P : (a + 1) * P],
-                    rhs=h_codes[:].bitcast(FP8X4),
-                    rhs_scale=h_plane[:],
-                    start=True,
-                    stop=True,
-                )
-                if last and a == 0:
-                    nc.scalar.copy(out=result[:, a, :], in_=bank[:, a, :])
-                if last and a == 1:
-                    nc.vector.tensor_copy(out=result[:, a, :], in_=bank[:, a, :])
-            if not last:
-                nc.scalar.copy(out=result[:], in_=bank[:])
-            nc.sync.dma_start(out=out_rows[:, :, s0 : s0 + width], in_=result[:])
+            return h_codes, h_plane
 
-        s0 = 0
-        waiting = None
-        for gi, width in enumerate(GROUPS):
-            h_bf = keep.tile([P, width, PACK], BF16, name=f"h_bf{gi}", align_bytes=64)
-            for lo in range(0, width, CHUNK):
-                hidden(s0 + lo, h_bf, lo)
-                if lo == 0 and waiting is not None:
-                    second(*waiting)
-            waiting = (s0, width, h_bf, gi)
-            s0 += width
-        second(*waiting)
+        def second(dst, a, h_codes, h_plane):
+            nc.tensor.matmul_mx(
+                out=dst,
+                lhsT=w2_codes[:, a * P : (a + 1) * P].bitcast(FP8X4),
+                lhsT_scale=w2_plane[:, a * P : (a + 1) * P],
+                rhs=h_codes[:].bitcast(FP8X4),
+                rhs_scale=h_plane[:],
+                start=True,
+                stop=True,
+            )
+
+        chunks = S // CHUNK
+        for c0 in range(0, chunks, 2):
+            h_pair = []
+            for c in (c0, c0 + 1):
+                h_bf = keep.tile([P, CHUNK, PACK], BF16, name=f"h_bf{c}", align_bytes=64)
+                hidden(c * CHUNK, h_bf, 0)
+                h_pair.append(h_bf)
+            quantized = [quantize_hidden(h_pair[u], c0 + u) for u in range(2)]
+            s0 = c0 * CHUNK
+            if c0 + 2 < chunks:
+                bank = out_psum.tile([P, N // P, 2 * CHUNK], F32, name="out_bank")
+                for u in range(2):
+                    for a in range(N // P):
+                        second(bank[:, a, u * CHUNK : (u + 1) * CHUNK], a, *quantized[u])
+                result = keep.tile([P, N // P, 2 * CHUNK], F32, name=f"result{c0}")
+                nc.scalar.copy(out=result[:], in_=bank[:])
+                nc.sync.dma_start(out=out_rows[:, :, s0 : s0 + 2 * CHUNK], in_=result[:])
+            else:
+                bank = out_psum.tile([P, N // P, CHUNK], F32, name="out_bank")
+                for a in range(N // P):
+                    second(bank[:, a, :], a, *quantized[0])
+                result = keep.tile([P, N // P, CHUNK], F32, name=f"result{c0}")
+                nc.scalar.copy(out=result[:], in_=bank[:])
+                nc.sync.dma_start(out=out_rows[:, :, s0 : s0 + CHUNK], in_=result[:])
+                result = keep.tile([P, N // P, CHUNK], F32, name=f"result{c0 + 1}")
+                for a, copy in enumerate((nc.scalar.copy, nc.vector.tensor_copy)):
+                    bank = out_psum.tile([P, CHUNK], F32, name="out_bank")
+                    second(bank[:], a, *quantized[1])
+                    copy(out=result[:, a, :], in_=bank[:])
+                nc.sync.dma_start(out=out_rows[:, :, s0 + CHUNK : s0 + 2 * CHUNK], in_=result[:])

@@ -16,70 +16,92 @@ ADD = mybir.AluOpType.add
 
 P = 128
 PACK = 4
+LIST_ROWS = 16
 CHUNK = 128
+PAIR = 2 * CHUNK
 GATHER = 512
-POS_LOADS = (256, 256, 256, 256)
+BANKS = 4
 
 
-def load_scale_rows(queues, plane, rows):
+def load_plane(nc, plane, rows):
     for q in range(4):
-        queues[q % len(queues)].dma_start(out=plane[32 * q : 32 * q + 4, :].bitcast(I32), in_=rows[4 * q : 4 * q + 4, :].bitcast(I32))
+        nc.sync.dma_start(
+            out=plane[32 * q : 32 * q + 4, :].bitcast(I32),
+            in_=rows[4 * q : 4 * q + 4, :].bitcast(I32),
+        )
+
+
+def load_codes(nc, codes, words):
+    nc.sync.dma_start(out=codes[:], in_=words.rearrange("p c j -> p (c j)").bitcast(I32))
+
+
+def lone_pass(nc, dst, stationary, moving):
+    nc.tensor.matmul_mx(
+        out=dst,
+        lhsT=stationary[0].bitcast(FP8X4),
+        lhsT_scale=stationary[1],
+        rhs=moving[0].bitcast(FP8X4),
+        rhs_scale=moving[1],
+        start=True,
+        stop=True,
+    )
 
 
 def tile_picked_embpos_none_p_kernel(tc, x_words, x_scales, w1, w2_words, w2_scales, pos, offs, out):
     nc = tc.nc
     with ExitStack() as ctx:
         keep = ctx.enter_context(tc.tile_pool(name="keep", bufs=1))
-        hid_psum = ctx.enter_context(tc.psum_pool(name="hid_psum", bufs=4))
-        out_psum = ctx.enter_context(tc.psum_pool(name="out_psum", bufs=4))
+        hid_psum = ctx.enter_context(tc.psum_pool(name="hid_psum", bufs=BANKS))
+        out_psum = ctx.enter_context(tc.psum_pool(name="out_psum", bufs=BANKS))
 
-        offsets = keep.tile([P, S // 16], U16, name="offsets")
-
-        table_scales = keep.tile([P, T], U8, name="table_scales", align_bytes=64)
-        nc.vector.memset(table_scales[:].bitcast(I32), 0)
+        offsets = keep.tile([P, S // LIST_ROWS], U16, name="offsets")
+        table_plane = keep.tile([P, T], U8, name="table_plane", align_bytes=64)
+        nc.vector.memset(table_plane[:].bitcast(I32), 0)
 
         w1_rows = w1.rearrange("(p j) c -> p j c", j=PACK)
         w1_raw = []
         for half in range(2):
-            raw = keep.tile([P, PACK, H // 2], F32, name=f"w1_raw{half}")
-            nc.sync.dma_start(out=raw[:], in_=w1_rows[:, :, half * (H // 2) : (half + 1) * (H // 2)])
+            raw = keep.tile([P, 2, H], F32, name=f"w1_raw{half}")
+            nc.sync.dma_start(out=raw[:], in_=w1_rows[:, 2 * half : 2 * half + 2, :])
             w1_raw.append(raw)
             if half == 0:
                 nc.sync.dma_start(offsets[:], offs)
-                load_scale_rows((nc.sync, nc.scalar), table_scales, x_scales[0])
-        table_words = keep.tile([P, T], I32, name="table_words", align_bytes=64)
-        nc.sync.dma_start(out=table_words[:], in_=x_words[0].rearrange("p c r -> p (c r)").bitcast(I32))
+                load_plane(nc, table_plane, x_scales[0])
+        table_codes = keep.tile([P, T], I32, name="table_codes", align_bytes=64)
+        load_codes(nc, table_codes, x_words[0])
+
         w2_codes = keep.tile([P, N], I32, name="w2_codes", align_bytes=64)
         w2_plane = keep.tile([P, N], U8, name="w2_plane", align_bytes=64)
         nc.gpsimd.memset(w2_plane[:].bitcast(I32), 0)
+
         pos_rows = pos.rearrange("(p t) s -> p t s", t=PACK)
         pos_sb = []
-        first = 0
-        for g, width in enumerate(POS_LOADS):
-            part = keep.tile([P, PACK, width], F32, name=f"pos{g}")
-            nc.sync.dma_start(out=part[:], in_=pos_rows[:, :, first : first + width])
-            pos_sb.extend(part[:, :, lo : lo + CHUNK] for lo in range(0, width, CHUNK))
-            first += width
-            if g == 1:
-                nc.sync.dma_start(out=w2_codes[:], in_=w2_words[0].rearrange("p c r -> p (c r)").bitcast(I32))
-                load_scale_rows((nc.sync,), w2_plane, w2_scales[0])
+        for pair in range(S // PAIR):
+            part = keep.tile([P, PACK, PAIR], F32, name=f"pos{pair}")
+            nc.sync.dma_start(out=part[:], in_=pos_rows[:, :, pair * PAIR : (pair + 1) * PAIR])
+            pos_sb.extend(part[:, :, lo : lo + CHUNK] for lo in range(0, PAIR, CHUNK))
+            if pair == 1:
+                load_codes(nc, w2_codes, w2_words[0])
+                load_plane(nc, w2_plane, w2_scales[0])
 
-        x_codes, x_plane = [], []
+        def list_slice(g):
+            return offsets[:, g * GATHER // LIST_ROWS : (g + 1) * GATHER // LIST_ROWS]
+
+        x_plane = []
         for g in range(S // GATHER):
             plane = keep.tile([P, GATHER], U8, name=f"x_plane{g}", align_bytes=64)
-            cols = slice(g * GATHER // 16, (g + 1) * GATHER // 16)
-            nc.vector.tensor_copy(out=plane[:], in_=table_scales[:].indirect(offsets[:, cols]))
+            nc.vector.tensor_copy(out=plane[:], in_=table_plane[:].indirect(list_slice(g)))
             x_plane.append(plane)
 
         w1_codes = keep.tile([P, H], U32, name="w1_codes", align_bytes=64)
         w1_plane = keep.tile([P, H], U8, name="w1_plane", align_bytes=64)
         w1_grouped = [
-            keep.tile([P, 2, P, PACK], BF16, name=f"w1_grouped{u}", tag=f"late{u}", align_bytes=64) for u in range(2)
+            keep.tile([P, 2, P, PACK], BF16, name=f"w1_grouped{u}", tag=f"shared{u}", align_bytes=64) for u in range(2)
         ]
         for half in range(2):
             for u in range(2):
                 nc.scalar.copy(
-                    out=w1_grouped[u][:, :, half * (P // 2) : (half + 1) * (P // 2), :].rearrange("p t m j -> p m j t"),
+                    out=w1_grouped[u][:, :, :, 2 * half : 2 * half + 2].rearrange("p t m j -> p m j t"),
                     in_=w1_raw[half][:].rearrange("p j (m t) -> p m j t", t=PACK)[:, :, :, 2 * u : 2 * u + 2],
                 )
         for u in range(2):
@@ -90,36 +112,29 @@ def tile_picked_embpos_none_p_kernel(tc, x_words, x_scales, w1, w2_words, w2_sca
                 in_=w1_grouped[u][:].rearrange("p t m j -> p (t m j)"),
             )
 
+        x_codes = []
         for g in range(S // GATHER):
-            codes = keep.tile([P, GATHER], U32, name=f"x_codes{g}", tag="late0" if g == 0 else "codes1", align_bytes=64)
-            cols = slice(g * GATHER // 16, (g + 1) * GATHER // 16)
-            nc.vector.tensor_copy(out=codes[:], in_=table_words[:].bitcast(U32).indirect(offsets[:, cols]))
+            codes = keep.tile([P, GATHER], U32, name=f"x_codes{g}", tag=f"shared{g}", align_bytes=64)
+            nc.vector.tensor_copy(out=codes[:], in_=table_codes[:].bitcast(U32).indirect(list_slice(g)))
             x_codes.append(codes)
 
-
-        out_rows = out.rearrange("(a p) s -> p a s", p=P)
-
-        def hidden(s0, h_bf, lo):
+        def hidden(c):
+            g, lo = divmod(c * CHUNK, GATHER)
+            picked = (x_codes[g][:, lo : lo + CHUNK], x_plane[g][:, lo : lo + CHUNK])
             bank = hid_psum.tile([P, PACK, CHUNK], F32, name="hid_bank")
-            g, c0 = divmod(s0, GATHER)
             for t in range(PACK):
-                nc.tensor.matmul_mx(
-                    out=bank[:, t, :],
-                    lhsT=w1_codes[:, t * P : (t + 1) * P].bitcast(FP8X4),
-                    lhsT_scale=w1_plane[:, t * P : (t + 1) * P],
-                    rhs=x_codes[g][:, c0 : c0 + CHUNK].bitcast(FP8X4),
-                    rhs_scale=x_plane[g][:, c0 : c0 + CHUNK],
-                    start=True,
-                    stop=True,
-                )
+                cols = slice(t * P, (t + 1) * P)
+                lone_pass(nc, bank[:, t, :], (w1_codes[:, cols], w1_plane[:, cols]), picked)
+            h_bf = keep.tile([P, CHUNK, PACK], BF16, name=f"h_bf{c}", align_bytes=64)
             nc.vector.tensor_tensor(
-                out=h_bf[:, lo : lo + CHUNK, :].rearrange("p (c i) t -> p c t i", i=2),
-                in0=bank[:].rearrange("p t (c i) -> p c t i", i=2),
-                in1=pos_sb[s0 // CHUNK].rearrange("p t (c i) -> p c t i", i=2),
+                out=h_bf[:].rearrange("p (d e) t -> p d t e", e=2),
+                in0=bank[:].rearrange("p t (d e) -> p d t e", e=2),
+                in1=pos_sb[c].rearrange("p t (d e) -> p d t e", e=2),
                 op=ADD,
             )
+            return h_bf
 
-        def quantize_hidden(h_bf, c):
+        def quantize_hidden(c, h_bf):
             h_codes = keep.tile([P, CHUNK], U32, name=f"h_codes{c}", align_bytes=64)
             h_plane = keep.tile([P, CHUNK], U8, name=f"h_plane{c}", align_bytes=64)
             nc.vector.quantize_mx(
@@ -127,46 +142,35 @@ def tile_picked_embpos_none_p_kernel(tc, x_words, x_scales, w1, w2_words, w2_sca
                 scales=h_plane[:],
                 in_=h_bf[:].rearrange("p s t -> p (s t)"),
             )
-            return h_codes, h_plane
+            return h_codes[:], h_plane[:]
 
-        def second(dst, a, h_codes, h_plane):
-            nc.tensor.matmul_mx(
-                out=dst,
-                lhsT=w2_codes[:, a * P : (a + 1) * P].bitcast(FP8X4),
-                lhsT_scale=w2_plane[:, a * P : (a + 1) * P],
-                rhs=h_codes[:].bitcast(FP8X4),
-                rhs_scale=h_plane[:],
-                start=True,
-                stop=True,
-            )
+        out_rows = out.rearrange("(a p) s -> p a s", p=P)
+        w2_tiles = [(w2_codes[:, a * P : (a + 1) * P], w2_plane[:, a * P : (a + 1) * P]) for a in range(N // P)]
+
+        def finish_together(c0, h_mx):
+            width = len(h_mx) * CHUNK
+            bank = out_psum.tile([P, N // P, width], F32, name="out_bank")
+            for n, moving in enumerate(h_mx):
+                for a, stationary in enumerate(w2_tiles):
+                    lone_pass(nc, bank[:, a, n * CHUNK : (n + 1) * CHUNK], stationary, moving)
+            result = keep.tile([P, N // P, width], F32, name=f"result{c0}")
+            nc.scalar.copy(out=result[:], in_=bank[:])
+            nc.sync.dma_start(out=out_rows[:, :, c0 * CHUNK : c0 * CHUNK + width], in_=result[:])
+
+        def finish_last(c, moving):
+            result = keep.tile([P, N // P, CHUNK], F32, name=f"result{c}")
+            for a, copy in enumerate((nc.scalar.copy, nc.vector.tensor_copy)):
+                bank = out_psum.tile([P, CHUNK], F32, name="out_bank")
+                lone_pass(nc, bank[:], w2_tiles[a], moving)
+                copy(out=result[:, a, :], in_=bank[:])
+            nc.sync.dma_start(out=out_rows[:, :, c * CHUNK : (c + 1) * CHUNK], in_=result[:])
 
         chunks = S // CHUNK
         for c0 in range(0, chunks, 2):
-            h_pair = []
-            for c in (c0, c0 + 1):
-                h_bf = keep.tile([P, CHUNK, PACK], BF16, name=f"h_bf{c}", align_bytes=64)
-                hidden(c * CHUNK, h_bf, 0)
-                h_pair.append(h_bf)
-            quantized = [quantize_hidden(h_pair[u], c0 + u) for u in range(2)]
-            s0 = c0 * CHUNK
+            h_pair = [hidden(c) for c in (c0, c0 + 1)]
+            h_mx = [quantize_hidden(c0 + n, h_bf) for n, h_bf in enumerate(h_pair)]
             if c0 + 2 < chunks:
-                bank = out_psum.tile([P, N // P, 2 * CHUNK], F32, name="out_bank")
-                for u in range(2):
-                    for a in range(N // P):
-                        second(bank[:, a, u * CHUNK : (u + 1) * CHUNK], a, *quantized[u])
-                result = keep.tile([P, N // P, 2 * CHUNK], F32, name=f"result{c0}")
-                nc.scalar.copy(out=result[:], in_=bank[:])
-                nc.sync.dma_start(out=out_rows[:, :, s0 : s0 + 2 * CHUNK], in_=result[:])
+                finish_together(c0, h_mx)
             else:
-                bank = out_psum.tile([P, N // P, CHUNK], F32, name="out_bank")
-                for a in range(N // P):
-                    second(bank[:, a, :], a, *quantized[0])
-                result = keep.tile([P, N // P, CHUNK], F32, name=f"result{c0}")
-                nc.scalar.copy(out=result[:], in_=bank[:])
-                nc.sync.dma_start(out=out_rows[:, :, s0 : s0 + CHUNK], in_=result[:])
-                result = keep.tile([P, N // P, CHUNK], F32, name=f"result{c0 + 1}")
-                for a, copy in enumerate((nc.scalar.copy, nc.vector.tensor_copy)):
-                    bank = out_psum.tile([P, CHUNK], F32, name="out_bank")
-                    second(bank[:], a, *quantized[1])
-                    copy(out=result[:, a, :], in_=bank[:])
-                nc.sync.dma_start(out=out_rows[:, :, s0 + CHUNK : s0 + 2 * CHUNK], in_=result[:])
+                finish_together(c0, h_mx[:1])
+                finish_last(c0 + 1, h_mx[1])

@@ -87,23 +87,25 @@ def tile_picked_embpos_none_p_kernel(tc, x_words, x_scales, w1, w2_words, w2_sca
         def list_slice(g):
             return offsets[:, g * GATHER // LIST_ROWS : (g + 1) * GATHER // LIST_ROWS]
 
-        x_plane = []
-        for g in range(S // GATHER):
-            plane = keep.tile([P, GATHER], U8, name=f"x_plane{g}", align_bytes=64)
-            nc.vector.tensor_copy(out=plane[:], in_=table_plane[:].indirect(list_slice(g)))
-            x_plane.append(plane)
+        x_plane = keep.tile([P, S], U8, name="x_plane", align_bytes=64)
+        nc.vector.tensor_copy(out=x_plane[:], in_=table_plane[:].indirect(offsets[:]))
 
         w1_codes = keep.tile([P, H], U32, name="w1_codes", align_bytes=64)
         w1_plane = keep.tile([P, H], U8, name="w1_plane", align_bytes=64)
         w1_grouped = [
             keep.tile([P, 2, P, PACK], BF16, name=f"w1_grouped{u}", tag=f"shared{u}", align_bytes=64) for u in range(2)
         ]
-        for half in range(2):
-            for u in range(2):
-                nc.scalar.copy(
-                    out=w1_grouped[u][:, :, :, 2 * half : 2 * half + 2].rearrange("p t m j -> p m j t"),
-                    in_=w1_raw[half][:].rearrange("p j (m t) -> p m j t", t=PACK)[:, :, :, 2 * u : 2 * u + 2],
-                )
+        def deal_w1(copy, half, u, m0, m1):
+            copy(
+                out=w1_grouped[u][:, :, m0:m1, 2 * half : 2 * half + 2].rearrange("p t m j -> p m j t"),
+                in_=w1_raw[half][:].rearrange("p j (m t) -> p m j t", t=PACK)[:, m0:m1, :, 2 * u : 2 * u + 2],
+            )
+
+        deal_w1(nc.scalar.copy, 0, 0, 0, P)
+        deal_w1(nc.vector.tensor_copy, 0, 1, 0, P)
+        deal_w1(nc.scalar.copy, 1, 0, 0, P)
+        deal_w1(nc.scalar.copy, 1, 1, 0, P // 2)
+        deal_w1(nc.vector.tensor_copy, 1, 1, P // 2, P)
         for u in range(2):
             cols = slice(u * 2 * P, (u + 1) * 2 * P)
             nc.vector.quantize_mx(
@@ -120,7 +122,7 @@ def tile_picked_embpos_none_p_kernel(tc, x_words, x_scales, w1, w2_words, w2_sca
 
         def hidden(c):
             g, lo = divmod(c * CHUNK, GATHER)
-            picked = (x_codes[g][:, lo : lo + CHUNK], x_plane[g][:, lo : lo + CHUNK])
+            picked = (x_codes[g][:, lo : lo + CHUNK], x_plane[:, c * CHUNK : (c + 1) * CHUNK])
             bank = hid_psum.tile([P, PACK, CHUNK], F32, name="hid_bank")
             for t in range(PACK):
                 cols = slice(t * P, (t + 1) * P)

@@ -20,6 +20,7 @@ LIST_ROWS = 16
 CHUNK = 128
 PAIR = 2 * CHUNK
 GATHER = 512
+POS_LOADS = (384, 256, 256, 128)
 BANKS = 4
 
 
@@ -76,11 +77,12 @@ def tile_picked_embpos_none_p_kernel(tc, x_words, x_scales, w1, w2_words, w2_sca
 
         pos_rows = pos.rearrange("(p t) s -> p t s", t=PACK)
         pos_sb = []
-        for pair in range(S // PAIR):
-            part = keep.tile([P, PACK, PAIR], F32, name=f"pos{pair}")
-            nc.sync.dma_start(out=part[:], in_=pos_rows[:, :, pair * PAIR : (pair + 1) * PAIR])
-            pos_sb.extend(part[:, :, lo : lo + CHUNK] for lo in range(0, PAIR, CHUNK))
-            if pair == 1:
+        for load, count in enumerate(POS_LOADS):
+            first = len(pos_sb) * CHUNK
+            part = keep.tile([P, PACK, count], F32, name=f"pos{load}")
+            nc.sync.dma_start(out=part[:], in_=pos_rows[:, :, first : first + count])
+            pos_sb.extend(part[:, :, lo : lo + CHUNK] for lo in range(0, count, CHUNK))
+            if load == 0:
                 load_codes(nc, w2_codes, w2_words[0])
                 load_plane(nc, w2_plane, w2_scales[0])
 
@@ -120,41 +122,39 @@ def tile_picked_embpos_none_p_kernel(tc, x_words, x_scales, w1, w2_words, w2_sca
             nc.vector.tensor_copy(out=codes[:], in_=table_codes[:].bitcast(U32).indirect(list_slice(g)))
             x_codes.append(codes)
 
-        def hidden(c):
+        def hidden(c, h_bf):
             g, lo = divmod(c * CHUNK, GATHER)
             picked = (x_codes[g][:, lo : lo + CHUNK], x_plane[:, c * CHUNK : (c + 1) * CHUNK])
             bank = hid_psum.tile([P, PACK, CHUNK], F32, name="hid_bank")
             for t in range(PACK):
                 cols = slice(t * P, (t + 1) * P)
                 lone_pass(nc, bank[:, t, :], (w1_codes[:, cols], w1_plane[:, cols]), picked)
-            h_bf = keep.tile([P, CHUNK, PACK], BF16, name=f"h_bf{c}", align_bytes=64)
             nc.vector.tensor_tensor(
-                out=h_bf[:].rearrange("p (d e) t -> p d t e", e=2),
+                out=h_bf.rearrange("p (d e) t -> p d t e", e=2),
                 in0=bank[:].rearrange("p t (d e) -> p d t e", e=2),
                 in1=pos_sb[c].rearrange("p t (d e) -> p d t e", e=2),
                 op=ADD,
             )
-            return h_bf
 
-        def quantize_hidden(c, h_bf):
-            h_codes = keep.tile([P, CHUNK], U32, name=f"h_codes{c}", align_bytes=64)
-            h_plane = keep.tile([P, CHUNK], U8, name=f"h_plane{c}", align_bytes=64)
+        def quantize_hidden(c0, h_bf):
+            width = h_bf.shape[1]
+            h_codes = keep.tile([P, width], U32, name=f"h_codes{c0}", align_bytes=64)
+            h_plane = keep.tile([P, width], U8, name=f"h_plane{c0}", align_bytes=64)
             nc.vector.quantize_mx(
                 out=h_codes[:].bitcast(FP8X4),
                 scales=h_plane[:],
-                in_=h_bf[:].rearrange("p s t -> p (s t)"),
+                in_=h_bf.rearrange("p s t -> p (s t)"),
             )
             return h_codes[:], h_plane[:]
 
         out_rows = out.rearrange("(a p) s -> p a s", p=P)
         w2_tiles = [(w2_codes[:, a * P : (a + 1) * P], w2_plane[:, a * P : (a + 1) * P]) for a in range(N // P)]
 
-        def finish_together(c0, h_mx):
-            width = len(h_mx) * CHUNK
+        def finish(c0, moving):
+            width = moving[0].shape[1]
             bank = out_psum.tile([P, N // P, width], F32, name="out_bank")
-            for n, moving in enumerate(h_mx):
-                for a, stationary in enumerate(w2_tiles):
-                    lone_pass(nc, bank[:, a, n * CHUNK : (n + 1) * CHUNK], stationary, moving)
+            for a, stationary in enumerate(w2_tiles):
+                lone_pass(nc, bank[:, a, :], stationary, moving)
             result = keep.tile([P, N // P, width], F32, name=f"result{c0}")
             nc.scalar.copy(out=result[:], in_=bank[:])
             nc.sync.dma_start(out=out_rows[:, :, c0 * CHUNK : c0 * CHUNK + width], in_=result[:])
@@ -168,11 +168,15 @@ def tile_picked_embpos_none_p_kernel(tc, x_words, x_scales, w1, w2_words, w2_sca
             nc.sync.dma_start(out=out_rows[:, :, c * CHUNK : (c + 1) * CHUNK], in_=result[:])
 
         chunks = S // CHUNK
-        for c0 in range(0, chunks, 2):
-            h_pair = [hidden(c) for c in (c0, c0 + 1)]
-            h_mx = [quantize_hidden(c0 + n, h_bf) for n, h_bf in enumerate(h_pair)]
-            if c0 + 2 < chunks:
-                finish_together(c0, h_mx)
-            else:
-                finish_together(c0, h_mx[:1])
-                finish_last(c0 + 1, h_mx[1])
+        h_pairs = [keep.tile([P, PAIR, PACK], BF16, name=f"h_bf{n}", align_bytes=64) for n in range(chunks // 2)]
+
+        def h_chunk(c):
+            return h_pairs[c // 2][:, c % 2 * CHUNK : (c % 2 + 1) * CHUNK, :]
+
+        for c in range(chunks):
+            hidden(c, h_chunk(c))
+            if c % 2 == 0 and c > 0:
+                finish(c - 2, quantize_hidden(c - 2, h_pairs[c // 2 - 1][:]))
+        last_two = [quantize_hidden(c, h_chunk(c)) for c in (chunks - 2, chunks - 1)]
+        finish(chunks - 2, last_two[0])
+        finish_last(chunks - 1, last_two[1])

@@ -122,17 +122,19 @@ def tile_picked_embpos_none_p_kernel(tc, x_words, x_scales, w1, w2_words, w2_sca
             nc.vector.tensor_copy(out=codes[:], in_=table_codes[:].bitcast(U32).indirect(list_slice(g)))
             x_codes.append(codes)
 
-        def hidden(c, h_bf):
-            g, lo = divmod(c * CHUNK, GATHER)
-            picked = (x_codes[g][:, lo : lo + CHUNK], x_plane[:, c * CHUNK : (c + 1) * CHUNK])
-            bank = hid_psum.tile([P, PACK, CHUNK], F32, name="hid_bank")
+        def hidden(first, h_bf):
+            width = h_bf.shape[1]
+            g, lo = divmod(first, GATHER)
+            picked = (x_codes[g][:, lo : lo + width], x_plane[:, first : first + width])
+            bank = hid_psum.tile([P, PACK, width], F32, name="hid_bank")
             for t in range(PACK):
                 cols = slice(t * P, (t + 1) * P)
                 lone_pass(nc, bank[:, t, :], (w1_codes[:, cols], w1_plane[:, cols]), picked)
+            c, lo = divmod(first, CHUNK)
             nc.vector.tensor_tensor(
                 out=h_bf.rearrange("p (d e) t -> p d t e", e=2),
                 in0=bank[:].rearrange("p t (d e) -> p d t e", e=2),
-                in1=pos_sb[c].rearrange("p t (d e) -> p d t e", e=2),
+                in1=pos_sb[c][:, :, lo : lo + width].rearrange("p t (d e) -> p d t e", e=2),
                 op=ADD,
             )
 
@@ -150,33 +152,49 @@ def tile_picked_embpos_none_p_kernel(tc, x_words, x_scales, w1, w2_words, w2_sca
         out_rows = out.rearrange("(a p) s -> p a s", p=P)
         w2_tiles = [(w2_codes[:, a * P : (a + 1) * P], w2_plane[:, a * P : (a + 1) * P]) for a in range(N // P)]
 
-        def finish(c0, moving):
-            width = moving[0].shape[1]
-            bank = out_psum.tile([P, N // P, width], F32, name="out_bank")
-            for a, stationary in enumerate(w2_tiles):
-                lone_pass(nc, bank[:, a, :], stationary, moving)
-            result = keep.tile([P, N // P, width], F32, name=f"result{c0}")
-            nc.scalar.copy(out=result[:], in_=bank[:])
-            nc.sync.dma_start(out=out_rows[:, :, c0 * CHUNK : c0 * CHUNK + width], in_=result[:])
+        def finish(first, runs):
+            total = sum(moving[0].shape[1] for moving, copy in runs)
+            result = keep.tile([P, N // P, total], F32, name=f"result{first}")
+            lo = 0
+            for moving, copy in runs:
+                width = moving[0].shape[1]
+                bank = out_psum.tile([P, N // P, width], F32, name="out_bank")
+                for a, stationary in enumerate(w2_tiles):
+                    lone_pass(nc, bank[:, a, :], stationary, moving)
+                copy(out=result[:, :, lo : lo + width], in_=bank[:])
+                lo += width
+            nc.sync.dma_start(out=out_rows[:, :, first : first + total], in_=result[:])
 
-        def finish_last(c, moving):
-            result = keep.tile([P, N // P, CHUNK], F32, name=f"result{c}")
-            for a, copy in enumerate((nc.scalar.copy, nc.vector.tensor_copy)):
-                bank = out_psum.tile([P, CHUNK], F32, name="out_bank")
+        h_pairs = [keep.tile([P, PAIR, PACK], BF16, name=f"h_bf{n}", align_bytes=64) for n in range(S // PAIR)]
+
+        def h_of(first, width):
+            n, lo = divmod(first, PAIR)
+            return h_pairs[n][:, lo : lo + width, :]
+
+        def add(first, width):
+            hidden(first, h_of(first, width))
+
+        def quantize(first, width):
+            return quantize_hidden(first, h_of(first, width))
+
+        scalar, vector = nc.scalar.copy, nc.vector.tensor_copy
+        C, half = CHUNK, CHUNK // 2
+        for c in (0, 1, 2):
+            add(c * C, C)
+        finish(0, [(quantize(0, PAIR), scalar)])
+        for c in (3, 4):
+            add(c * C, C)
+        pair = quantize(2 * C, PAIR)
+        add(5 * C, C)
+        finish(2 * C, [(pair, scalar), (quantize(4 * C, C), scalar)])
+        add(6 * C, C)
+        finish(5 * C, [(quantize(5 * C, C), scalar)])
+        add(7 * C, C)
+        six, seven = quantize(6 * C, C), quantize(7 * C, C)
+        for c, moving in ((6, six), (7, seven)):
+            result = keep.tile([P, N // P, C], F32, name=f"result{c * C}")
+            for a, copy in enumerate((scalar, vector)):
+                bank = out_psum.tile([P, C], F32, name="out_bank")
                 lone_pass(nc, bank[:], w2_tiles[a], moving)
                 copy(out=result[:, a, :], in_=bank[:])
-            nc.sync.dma_start(out=out_rows[:, :, c * CHUNK : (c + 1) * CHUNK], in_=result[:])
-
-        chunks = S // CHUNK
-        h_pairs = [keep.tile([P, PAIR, PACK], BF16, name=f"h_bf{n}", align_bytes=64) for n in range(chunks // 2)]
-
-        def h_chunk(c):
-            return h_pairs[c // 2][:, c % 2 * CHUNK : (c % 2 + 1) * CHUNK, :]
-
-        for c in range(chunks):
-            hidden(c, h_chunk(c))
-            if c % 2 == 0 and c > 0:
-                finish(c - 2, quantize_hidden(c - 2, h_pairs[c // 2 - 1][:]))
-        last_two = [quantize_hidden(c, h_chunk(c)) for c in (chunks - 2, chunks - 1)]
-        finish(chunks - 2, last_two[0])
-        finish_last(chunks - 1, last_two[1])
+            nc.sync.dma_start(out=out_rows[:, :, c * C : (c + 1) * C], in_=result[:])

@@ -20,8 +20,6 @@ LIST_ROWS = 16
 CHUNK = 128
 PAIR = 2 * CHUNK
 GATHER = 512
-POS_LOADS = (384, 256, 256, 128)
-BANKS = 4
 
 
 def load_plane(nc, plane, rows):
@@ -52,8 +50,8 @@ def tile_picked_embpos_none_p_kernel(tc, x_words, x_scales, w1, w2_words, w2_sca
     nc = tc.nc
     with ExitStack() as ctx:
         keep = ctx.enter_context(tc.tile_pool(name="keep", bufs=1))
-        hid_psum = ctx.enter_context(tc.psum_pool(name="hid_psum", bufs=BANKS))
-        out_psum = ctx.enter_context(tc.psum_pool(name="out_psum", bufs=BANKS))
+        hid_psum = ctx.enter_context(tc.psum_pool(name="hid_psum", bufs=4))
+        out_psum = ctx.enter_context(tc.psum_pool(name="out_psum", bufs=4))
 
         offsets = keep.tile([P, S // LIST_ROWS], U16, name="offsets")
         table_plane = keep.tile([P, T], U8, name="table_plane", align_bytes=64)
@@ -76,13 +74,13 @@ def tile_picked_embpos_none_p_kernel(tc, x_words, x_scales, w1, w2_words, w2_sca
         nc.gpsimd.memset(w2_plane[:].bitcast(I32), 0)
 
         pos_rows = pos.rearrange("(p t) s -> p t s", t=PACK)
-        pos_sb = []
-        for load, count in enumerate(POS_LOADS):
-            first = len(pos_sb) * CHUNK
-            part = keep.tile([P, PACK, count], F32, name=f"pos{load}")
-            nc.sync.dma_start(out=part[:], in_=pos_rows[:, :, first : first + count])
-            pos_sb.extend(part[:, :, lo : lo + CHUNK] for lo in range(0, count, CHUNK))
-            if load == 0:
+        pos_sb = {}
+        for load, (c0, count) in enumerate(((4, 2), (6, 2), (2, 2), (0, 2))):
+            part = keep.tile([P, PACK, count * CHUNK], F32, name=f"pos{load}")
+            nc.sync.dma_start(out=part[:], in_=pos_rows[:, :, c0 * CHUNK : (c0 + count) * CHUNK])
+            for n in range(count):
+                pos_sb[c0 + n] = part[:, :, n * CHUNK : (n + 1) * CHUNK]
+            if load == 2:
                 load_codes(nc, w2_codes, w2_words[0])
                 load_plane(nc, w2_plane, w2_scales[0])
 
@@ -116,27 +114,32 @@ def tile_picked_embpos_none_p_kernel(tc, x_words, x_scales, w1, w2_words, w2_sca
                 in_=w1_grouped[u][:].rearrange("p t m j -> p (t m j)"),
             )
 
-        x_codes = []
-        for g in range(S // GATHER):
-            codes = keep.tile([P, GATHER], U32, name=f"x_codes{g}", tag=f"shared{g}", align_bytes=64)
-            nc.vector.tensor_copy(out=codes[:], in_=table_codes[:].bitcast(U32).indirect(list_slice(g)))
-            x_codes.append(codes)
+        x_codes = {}
+        for g, (first, count) in enumerate(((512, 256), (768, 256), (0, 512))):
+            codes = keep.tile([P, count], U32, name=f"x_codes{g}", tag=f"shared{g}", align_bytes=64)
+            entries = offsets[:, first // LIST_ROWS : (first + count) // LIST_ROWS]
+            nc.vector.tensor_copy(out=codes[:], in_=table_codes[:].bitcast(U32).indirect(entries))
+            for lo in range(0, count, CHUNK):
+                x_codes[(first + lo) // CHUNK] = codes[:, lo : lo + CHUNK]
 
-        def hidden(first, h_bf):
-            width = h_bf.shape[1]
-            g, lo = divmod(first, GATHER)
-            picked = (x_codes[g][:, lo : lo + width], x_plane[:, first : first + width])
-            bank = hid_psum.tile([P, PACK, width], F32, name="hid_bank")
+        def product(c):
+            picked = (x_codes[c], x_plane[:, c * CHUNK : (c + 1) * CHUNK])
+            bank = hid_psum.tile([P, PACK, CHUNK], F32, name="hid_bank")
             for t in range(PACK):
                 cols = slice(t * P, (t + 1) * P)
                 lone_pass(nc, bank[:, t, :], (w1_codes[:, cols], w1_plane[:, cols]), picked)
-            c, lo = divmod(first, CHUNK)
-            nc.vector.tensor_tensor(
+            return bank
+
+        def add_pos(engine, c, summand, h_bf):
+            engine.tensor_tensor(
                 out=h_bf.rearrange("p (d e) t -> p d t e", e=2),
-                in0=bank[:].rearrange("p t (d e) -> p d t e", e=2),
-                in1=pos_sb[c][:, :, lo : lo + width].rearrange("p t (d e) -> p d t e", e=2),
+                in0=summand[:].rearrange("p t (d e) -> p d t e", e=2),
+                in1=pos_sb[c].rearrange("p t (d e) -> p d t e", e=2),
                 op=ADD,
             )
+
+        def add_on_vector(c, bank, h_bf):
+            add_pos(nc.vector, c, bank, h_bf)
 
         def quantize_hidden(c0, h_bf):
             width = h_bf.shape[1]
@@ -165,33 +168,29 @@ def tile_picked_embpos_none_p_kernel(tc, x_words, x_scales, w1, w2_words, w2_sca
                 lo += width
             nc.sync.dma_start(out=out_rows[:, :, first : first + total], in_=result[:])
 
-        h_pairs = [keep.tile([P, PAIR, PACK], BF16, name=f"h_bf{n}", align_bytes=64) for n in range(S // PAIR)]
-
-        def h_of(first, width):
-            n, lo = divmod(first, PAIR)
-            return h_pairs[n][:, lo : lo + width, :]
-
-        def add(first, width):
-            hidden(first, h_of(first, width))
-
-        def quantize(first, width):
-            return quantize_hidden(first, h_of(first, width))
+        def h_tile(c0, count):
+            return keep.tile([P, count * CHUNK, PACK], BF16, name=f"h_bf{c0}", align_bytes=64)
 
         scalar, vector = nc.scalar.copy, nc.vector.tensor_copy
-        C, half = CHUNK, CHUNK // 2
-        for c in (0, 1, 2):
-            add(c * C, C)
-        finish(0, [(quantize(0, PAIR), scalar)])
-        for c in (3, 4):
-            add(c * C, C)
-        pair = quantize(2 * C, PAIR)
-        add(5 * C, C)
-        finish(2 * C, [(pair, scalar), (quantize(4 * C, C), scalar)])
-        add(6 * C, C)
-        finish(5 * C, [(quantize(5 * C, C), scalar)])
-        add(7 * C, C)
-        six, seven = quantize(6 * C, C), quantize(7 * C, C)
-        for c, moving in ((6, six), (7, seven)):
+        C = CHUNK
+        h34, h56, h7, h2, h0, h1 = h_tile(3, 2), h_tile(5, 2), h_tile(7, 1), h_tile(2, 1), h_tile(0, 1), h_tile(1, 1)
+        plain = keep.tile([P, PACK, CHUNK], F32, name="plain")
+        nc.scalar.copy(out=plain[:], in_=product(4)[:])
+        add_pos(nc.gpsimd, 4, plain, h34[:, C:, :])
+        banks = {c: product(c) for c in (5, 6, 7)}
+        add_on_vector(5, banks[5], h56[:, :C, :])
+        add_on_vector(6, banks[6], h56[:, C:, :])
+        add_on_vector(7, banks[7], h7[:])
+        mx56 = quantize_hidden(5, h56[:])
+        add_on_vector(3, product(3), h34[:, :C, :])
+        finish(5 * C, [(mx56, scalar), (quantize_hidden(7, h7[:]), scalar)])
+        add_on_vector(2, product(2), h2[:])
+        finish(3 * C, [(quantize_hidden(3, h34[:]), scalar)])
+        add_on_vector(0, product(0), h0[:])
+        finish(2 * C, [(quantize_hidden(2, h2[:]), scalar)])
+        add_on_vector(1, product(1), h1[:])
+        last = [quantize_hidden(0, h0[:]), quantize_hidden(1, h1[:])]
+        for c, moving in enumerate(last):
             result = keep.tile([P, N // P, C], F32, name=f"result{c * C}")
             for a, copy in enumerate((scalar, vector)):
                 bank = out_psum.tile([P, C], F32, name="out_bank")

@@ -74,18 +74,14 @@ def tile_picked_embpos_none_p_kernel(tc, x_words, x_scales, w1, w2_words, w2_sca
         nc.gpsimd.memset(w2_plane[:].bitcast(I32), 0)
 
         pos_rows = pos.rearrange("(p t) s -> p t s", t=PACK)
-        pos_sb = {}
-        for load, (c0, count) in enumerate(((4, 2), (6, 2), (2, 2), (0, 2))):
-            part = keep.tile([P, PACK, count * CHUNK], F32, name=f"pos{load}")
-            nc.sync.dma_start(out=part[:], in_=pos_rows[:, :, c0 * CHUNK : (c0 + count) * CHUNK])
-            for n in range(count):
-                pos_sb[c0 + n] = part[:, :, n * CHUNK : (n + 1) * CHUNK]
-            if load == 2:
+        pos_parts = []
+        for load, (first, count) in enumerate(((0, 512), (512, 320), (832, 192))):
+            part = keep.tile([P, PACK, count], F32, name=f"pos{load}")
+            nc.sync.dma_start(out=part[:], in_=pos_rows[:, :, first : first + count])
+            pos_parts.append((first, count, part))
+            if load == 1:
                 load_codes(nc, w2_codes, w2_words[0])
                 load_plane(nc, w2_plane, w2_scales[0])
-
-        def list_slice(g):
-            return offsets[:, g * GATHER // LIST_ROWS : (g + 1) * GATHER // LIST_ROWS]
 
         x_plane = keep.tile([P, S], U8, name="x_plane", align_bytes=64)
         nc.vector.tensor_copy(out=x_plane[:], in_=table_plane[:].indirect(offsets[:]))
@@ -114,41 +110,58 @@ def tile_picked_embpos_none_p_kernel(tc, x_words, x_scales, w1, w2_words, w2_sca
                 in_=w1_grouped[u][:].rearrange("p t m j -> p (t m j)"),
             )
 
-        x_codes = {}
-        for g, (first, count) in enumerate(((512, 256), (768, 256), (0, 512))):
+        x_parts = []
+        for g, (first, count) in enumerate(((256, 256), (0, 256), (512, 512))):
             codes = keep.tile([P, count], U32, name=f"x_codes{g}", tag=f"shared{g}", align_bytes=64)
             entries = offsets[:, first // LIST_ROWS : (first + count) // LIST_ROWS]
             nc.vector.tensor_copy(out=codes[:], in_=table_codes[:].bitcast(U32).indirect(entries))
-            for lo in range(0, count, CHUNK):
-                x_codes[(first + lo) // CHUNK] = codes[:, lo : lo + CHUNK]
+            x_parts.append((first, count, codes))
 
-        def product(c):
-            picked = (x_codes[c], x_plane[:, c * CHUNK : (c + 1) * CHUNK])
-            bank = hid_psum.tile([P, PACK, CHUNK], F32, name="hid_bank")
+        def holder(parts, first):
+            return [(tile, first - lo) for lo, count, tile in parts if lo <= first < lo + count][0]
+
+        def product(first, width, pool=hid_psum, name="hid_bank"):
+            codes, lo = holder(x_parts, first)
+            picked = (codes[:, lo : lo + width], x_plane[:, first : first + width])
+            bank = pool.tile([P, PACK, width], F32, name=name)
             for t in range(PACK):
                 cols = slice(t * P, (t + 1) * P)
                 lone_pass(nc, bank[:, t, :], (w1_codes[:, cols], w1_plane[:, cols]), picked)
             return bank
 
-        def add_pos(engine, c, summand, h_bf):
+        h_parts = []
+
+        def h_tile(first, count):
+            h_parts.append((first, count, keep.tile([P, count, PACK], BF16, name=f"h_bf{first}", tag=f"h_bf{first}", align_bytes=64)))
+
+        def add_pos(engine, first, summand):
+            width = summand.shape[2]
+            part, lo = holder(pos_parts, first)
+            h_bf, at = holder(h_parts, first)
             engine.tensor_tensor(
-                out=h_bf.rearrange("p (d e) t -> p d t e", e=2),
+                out=h_bf[:, at : at + width, :].rearrange("p (d e) t -> p d t e", e=2),
                 in0=summand[:].rearrange("p t (d e) -> p d t e", e=2),
-                in1=pos_sb[c].rearrange("p t (d e) -> p d t e", e=2),
+                in1=part[:, :, lo : lo + width].rearrange("p t (d e) -> p d t e", e=2),
                 op=ADD,
             )
 
-        def add_on_vector(c, bank, h_bf):
-            add_pos(nc.vector, c, bank, h_bf)
+        def on_vector(first, width):
+            add_pos(nc.vector, first, product(first, width))
 
-        def quantize_hidden(c0, h_bf):
+        def on_gpsimd(first, width):
+            plain = keep.tile([P, PACK, width], F32, name=f"plain{first}")
+            nc.scalar.copy(out=plain[:], in_=product(first, width)[:])
+            add_pos(nc.gpsimd, first, plain)
+
+        def quantize(first):
+            h_bf = holder(h_parts, first)[0]
             width = h_bf.shape[1]
-            h_codes = keep.tile([P, width], U32, name=f"h_codes{c0}", align_bytes=64)
-            h_plane = keep.tile([P, width], U8, name=f"h_plane{c0}", align_bytes=64)
+            h_codes = keep.tile([P, width], U32, name=f"h_codes{first}", align_bytes=64)
+            h_plane = keep.tile([P, width], U8, name=f"h_plane{first}", align_bytes=64)
             nc.vector.quantize_mx(
                 out=h_codes[:].bitcast(FP8X4),
                 scales=h_plane[:],
-                in_=h_bf.rearrange("p s t -> p (s t)"),
+                in_=h_bf[:].rearrange("p s t -> p (s t)"),
             )
             return h_codes[:], h_plane[:]
 
@@ -168,32 +181,36 @@ def tile_picked_embpos_none_p_kernel(tc, x_words, x_scales, w1, w2_words, w2_sca
                 lo += width
             nc.sync.dma_start(out=out_rows[:, :, first : first + total], in_=result[:])
 
-        def h_tile(c0, count):
-            return keep.tile([P, count * CHUNK, PACK], BF16, name=f"h_bf{c0}", align_bytes=64)
-
         scalar, vector = nc.scalar.copy, nc.vector.tensor_copy
-        C = CHUNK
-        h34, h56, h7, h2, h0, h1 = h_tile(3, 2), h_tile(5, 2), h_tile(7, 1), h_tile(2, 1), h_tile(0, 1), h_tile(1, 1)
-        plain = keep.tile([P, PACK, CHUNK], F32, name="plain")
-        nc.scalar.copy(out=plain[:], in_=product(4)[:])
-        add_pos(nc.gpsimd, 4, plain, h34[:, C:, :])
-        banks = {c: product(c) for c in (5, 6, 7)}
-        add_on_vector(5, banks[5], h56[:, :C, :])
-        add_on_vector(6, banks[6], h56[:, C:, :])
-        add_on_vector(7, banks[7], h7[:])
-        mx56 = quantize_hidden(5, h56[:])
-        add_on_vector(3, product(3), h34[:, :C, :])
-        finish(5 * C, [(mx56, scalar), (quantize_hidden(7, h7[:]), scalar)])
-        add_on_vector(2, product(2), h2[:])
-        finish(3 * C, [(quantize_hidden(3, h34[:]), scalar)])
-        add_on_vector(0, product(0), h0[:])
-        finish(2 * C, [(quantize_hidden(2, h2[:]), scalar)])
-        add_on_vector(1, product(1), h1[:])
-        last = [quantize_hidden(0, h0[:]), quantize_hidden(1, h1[:])]
-        for c, moving in enumerate(last):
-            result = keep.tile([P, N // P, C], F32, name=f"result{c * C}")
+
+        def finish_split(first, moving):
+            width = moving[0].shape[1]
+            result = keep.tile([P, N // P, width], F32, name=f"result{first}")
             for a, copy in enumerate((scalar, vector)):
-                bank = out_psum.tile([P, C], F32, name="out_bank")
+                bank = out_psum.tile([P, width], F32, name="out_bank")
                 lone_pass(nc, bank[:], w2_tiles[a], moving)
                 copy(out=result[:, a, :], in_=bank[:])
-            nc.sync.dma_start(out=out_rows[:, :, c * C : (c + 1) * C], in_=result[:])
+            nc.sync.dma_start(out=out_rows[:, :, first : first + width], in_=result[:])
+
+        for first, count in ((0, 256), (256, 256), (512, 128), (704, 128), (832, 128), (960, 64)):
+            h_tile(first, count)
+        on_gpsimd(384, 128)
+        for first in (0, 128, 256):
+            on_vector(first, 128)
+        plain = keep.tile([P, PACK, 64], F32, name="plain640")
+        nc.scalar.copy(out=plain[:], in_=product(640, 64, out_psum, "out_bank")[:])
+        pairs = [quantize(0), quantize(256)]
+        h_parts.append((640, 64, keep.tile([P, 64, PACK], BF16, name="h_bf640", tag="h_bf256", align_bytes=64)))
+        add_pos(nc.gpsimd, 640, plain)
+        on_vector(512, 128)
+        finish(0, [(pairs[0], scalar)])
+        finish(256, [(pairs[1], scalar)])
+        on_vector(704, 128)
+        four = quantize(512)
+        finish(512, [(four, scalar), (quantize(640), scalar)])
+        on_vector(832, 128)
+        finish(704, [(quantize(704), scalar)])
+        on_vector(960, 64)
+        last = [quantize(832), quantize(960)]
+        finish_split(832, last[0])
+        finish_split(960, last[1])

@@ -148,10 +148,21 @@ def tile_picked_embpos_none_p_kernel(tc, x_words, x_scales, w1, w2_words, w2_sca
         def on_vector(first, width):
             add_pos(nc.vector, first, product(first, width))
 
-        def on_gpsimd(first, width):
-            plain = keep.tile([P, PACK, width], F32, name=f"plain{first}")
-            nc.scalar.copy(out=plain[:], in_=product(first, width)[:])
-            add_pos(nc.gpsimd, first, plain)
+        def out_of_psum(first, bank):
+            plain = keep.tile([P, bank.shape[2] // 4, PACK, 4], F32, name=f"plain{first}")
+            nc.scalar.copy(out=plain[:], in_=bank[:].rearrange("p t (d e) -> p d t e", e=4))
+            return plain
+
+        def on_gpsimd(first, plain):
+            width = 4 * plain.shape[1]
+            part, lo = holder(pos_parts, first)
+            h_bf, at = holder(h_parts, first)
+            nc.gpsimd.tensor_tensor(
+                out=h_bf[:, at : at + width, :].rearrange("p (d e) t -> p d t e", e=4),
+                in0=plain[:],
+                in1=part[:, :, lo : lo + width].rearrange("p t (d e) -> p d t e", e=4),
+                op=ADD,
+            )
 
         def quantize(first):
             h_bf = holder(h_parts, first)[0]
@@ -194,14 +205,13 @@ def tile_picked_embpos_none_p_kernel(tc, x_words, x_scales, w1, w2_words, w2_sca
 
         for first, count in ((0, 256), (256, 256), (512, 128), (704, 128), (832, 128), (960, 64)):
             h_tile(first, count)
-        on_gpsimd(384, 128)
+        on_gpsimd(384, out_of_psum(384, product(384, 128)))
         for first in (0, 128, 256):
             on_vector(first, 128)
-        plain = keep.tile([P, PACK, 64], F32, name="plain640")
-        nc.scalar.copy(out=plain[:], in_=product(640, 64, out_psum, "out_bank")[:])
+        plain = out_of_psum(640, product(640, 64, out_psum, "out_bank"))
         pairs = [quantize(0), quantize(256)]
         h_parts.append((640, 64, keep.tile([P, 64, PACK], BF16, name="h_bf640", tag="h_bf256", align_bytes=64)))
-        add_pos(nc.gpsimd, 640, plain)
+        on_gpsimd(640, plain)
         on_vector(512, 128)
         finish(0, [(pairs[0], scalar)])
         finish(256, [(pairs[1], scalar)])

@@ -194,15 +194,6 @@ def tile_picked_embpos_none_p_kernel(tc, x_words, x_scales, w1, w2_words, w2_sca
 
         scalar, vector = nc.scalar.copy, nc.vector.tensor_copy
 
-        def finish_split(first, moving):
-            width = moving[0].shape[1]
-            result = keep.tile([P, N // P, width], F32, name=f"result{first}")
-            for a, copy in enumerate((scalar, vector)):
-                bank = out_psum.tile([P, width], F32, name="out_bank")
-                lone_pass(nc, bank[:], w2_tiles[a], moving)
-                copy(out=result[:, a, :], in_=bank[:])
-            nc.sync.dma_start(out=out_rows[:, :, first : first + width], in_=result[:])
-
         for first, count in ((0, 256), (256, 256), (512, 128), (704, 128), (832, 128), (960, 64)):
             h_tile(first, count)
         on_gpsimd(384, out_of_psum(384, product(384, 128)))
@@ -210,7 +201,7 @@ def tile_picked_embpos_none_p_kernel(tc, x_words, x_scales, w1, w2_words, w2_sca
             on_vector(first, 128)
         plain = out_of_psum(640, product(640, 64, out_psum, "out_bank"))
         pairs = [quantize(0), quantize(256)]
-        h_parts.append((640, 64, keep.tile([P, 64, PACK], BF16, name="h_bf640", tag="h_bf256", align_bytes=64)))
+        h_parts.append((640, 64, keep.tile([P, 64, PACK], BF16, name="h_bf640", tag="h_bf0", align_bytes=64)))
         on_gpsimd(640, plain)
         on_vector(512, 128)
         finish(0, [(pairs[0], scalar)])
@@ -222,5 +213,11 @@ def tile_picked_embpos_none_p_kernel(tc, x_words, x_scales, w1, w2_words, w2_sca
         finish(704, [(quantize(704), scalar)])
         on_vector(960, 64)
         last = [quantize(832), quantize(960)]
-        finish_split(832, last[0])
-        finish_split(960, last[1])
+        result = keep.tile([P, N // P, 192], F32, name="result832")
+        for lo, moving in ((0, last[0]), (128, last[1])):
+            width = moving[0].shape[1]
+            for a, copy in enumerate((scalar, vector)):
+                bank = out_psum.tile([P, width], F32, name="out_bank")
+                lone_pass(nc, bank[:], w2_tiles[a], moving)
+                copy(out=result[:, a, lo : lo + width], in_=bank[:])
+        nc.sync.dma_start(out=out_rows[:, :, 832:], in_=result[:])

@@ -75,7 +75,7 @@ def tile_picked_embpos_none_p_kernel(tc, x_words, x_scales, w1, w2_words, w2_sca
 
         pos_rows = pos.rearrange("(p t) s -> p t s", t=PACK)
         pos_parts = []
-        for load, (first, count) in enumerate(((0, 512), (512, 320), (832, 192))):
+        for load, (first, count) in enumerate(((0, 512), (512, 256), (768, 256))):
             part = keep.tile([P, PACK, count], F32, name=f"pos{load}")
             nc.sync.dma_start(out=part[:], in_=pos_rows[:, :, first : first + count])
             pos_parts.append((first, count, part))
@@ -164,15 +164,14 @@ def tile_picked_embpos_none_p_kernel(tc, x_words, x_scales, w1, w2_words, w2_sca
                 op=ADD,
             )
 
-        def quantize(first):
-            h_bf = holder(h_parts, first)[0]
-            width = h_bf.shape[1]
+        def quantize(first, width):
+            h_bf, at = holder(h_parts, first)
             h_codes = keep.tile([P, width], U32, name=f"h_codes{first}", align_bytes=64)
             h_plane = keep.tile([P, width], U8, name=f"h_plane{first}", align_bytes=64)
             nc.vector.quantize_mx(
                 out=h_codes[:].bitcast(FP8X4),
                 scales=h_plane[:],
-                in_=h_bf[:].rearrange("p s t -> p (s t)"),
+                in_=h_bf[:, at : at + width, :].rearrange("p s t -> p (s t)"),
             )
             return h_codes[:], h_plane[:]
 
@@ -194,30 +193,28 @@ def tile_picked_embpos_none_p_kernel(tc, x_words, x_scales, w1, w2_words, w2_sca
 
         scalar, vector = nc.scalar.copy, nc.vector.tensor_copy
 
-        for first, count in ((0, 256), (256, 256), (512, 128), (704, 128), (832, 128), (960, 64)):
+        for first, count in ((0, 256), (256, 256), (576, 192), (768, 128), (896, 128)):
             h_tile(first, count)
         on_gpsimd(384, out_of_psum(384, product(384, 128)))
         for first in (0, 128, 256):
             on_vector(first, 128)
-        plain = out_of_psum(640, product(640, 64, out_psum, "out_bank"))
-        pairs = [quantize(0), quantize(256)]
-        h_parts.append((640, 64, keep.tile([P, 64, PACK], BF16, name="h_bf640", tag="h_bf0", align_bytes=64)))
-        on_gpsimd(640, plain)
-        on_vector(512, 128)
+        plain = out_of_psum(512, product(512, 64, out_psum, "out_bank"))
+        pairs = [quantize(0, 256), quantize(256, 256)]
+        h_parts.append((512, 64, keep.tile([P, 64, PACK], BF16, name="h_bf512", tag="h_bf0", align_bytes=64)))
+        on_gpsimd(512, plain)
+        on_vector(576, 128)
         finish(0, [(pairs[0], scalar)])
         finish(256, [(pairs[1], scalar)])
-        on_vector(704, 128)
-        four = quantize(512)
-        finish(512, [(four, scalar), (quantize(640), scalar)])
-        on_vector(832, 128)
-        finish(704, [(quantize(704), scalar)])
-        on_vector(960, 64)
-        last = [quantize(832), quantize(960)]
-        result = keep.tile([P, N // P, 192], F32, name="result832")
-        for lo, moving in ((0, last[0]), (128, last[1])):
-            width = moving[0].shape[1]
+        on_vector(704, 64)
+        on_vector(768, 128)
+        third = [quantize(576, 128), quantize(704, 64), quantize(512, 64)]
+        finish(512, [(third[2], scalar), (third[0], scalar), (third[1], scalar)])
+        on_vector(896, 128)
+        for first in (768, 896):
+            moving = quantize(first, 128)
+            result = keep.tile([P, N // P, 128], F32, name=f"result{first}")
             for a, copy in enumerate((scalar, vector)):
-                bank = out_psum.tile([P, width], F32, name="out_bank")
+                bank = out_psum.tile([P, 128], F32, name="out_bank")
                 lone_pass(nc, bank[:], w2_tiles[a], moving)
-                copy(out=result[:, a, lo : lo + width], in_=bank[:])
-        nc.sync.dma_start(out=out_rows[:, :, 832:], in_=result[:])
+                copy(out=result[:, a, :], in_=bank[:])
+            nc.sync.dma_start(out=out_rows[:, :, first : first + 128], in_=result[:])

@@ -164,15 +164,17 @@ def tile_picked_embpos_none_p_kernel(tc, x_words, x_scales, w1, w2_words, w2_sca
                 op=ADD,
             )
 
-        def quantize(first, width):
-            h_bf, at = holder(h_parts, first)
-            h_codes = keep.tile([P, width], U32, name=f"h_codes{first}", align_bytes=64)
-            h_plane = keep.tile([P, width], U8, name=f"h_plane{first}", align_bytes=64)
-            nc.vector.quantize_mx(
-                out=h_codes[:].bitcast(FP8X4),
-                scales=h_plane[:],
-                in_=h_bf[:, at : at + width, :].rearrange("p s t -> p (s t)"),
-            )
+        def quantize(first, runs):
+            total = sum(width for lo, width in runs)
+            h_codes = keep.tile([P, total], U32, name=f"h_codes{first}", align_bytes=64)
+            h_plane = keep.tile([P, total], U8, name=f"h_plane{first}", align_bytes=64)
+            for lo, width in runs:
+                h_bf, at = holder(h_parts, first + lo)
+                nc.vector.quantize_mx(
+                    out=h_codes[:, lo : lo + width].bitcast(FP8X4),
+                    scales=h_plane[:, lo : lo + width],
+                    in_=h_bf[:, at : at + width, :].rearrange("p s t -> p (s t)"),
+                )
             return h_codes[:], h_plane[:]
 
         out_rows = out.rearrange("(a p) s -> p a s", p=P)
@@ -193,13 +195,22 @@ def tile_picked_embpos_none_p_kernel(tc, x_words, x_scales, w1, w2_words, w2_sca
 
         scalar, vector = nc.scalar.copy, nc.vector.tensor_copy
 
-        for first, count in ((0, 256), (256, 256), (576, 192), (768, 128), (896, 128)):
+        def finish_shared(first, moving):
+            width = moving[0].shape[1]
+            result = keep.tile([P, N // P, width], F32, name=f"result{first}")
+            for a, copy in enumerate((scalar, vector)):
+                bank = out_psum.tile([P, width], F32, name="out_bank")
+                lone_pass(nc, bank[:], w2_tiles[a], moving)
+                copy(out=result[:, a, :], in_=bank[:])
+            nc.sync.dma_start(out=out_rows[:, :, first : first + width], in_=result[:])
+
+        for first, count in ((0, 256), (256, 128), (384, 128), (576, 192), (768, 128)):
             h_tile(first, count)
         on_gpsimd(384, out_of_psum(384, product(384, 128)))
         for first in (0, 128, 256):
             on_vector(first, 128)
         plain = out_of_psum(512, product(512, 64, out_psum, "out_bank"))
-        pairs = [quantize(0, 256), quantize(256, 256)]
+        pairs = [quantize(0, [(0, 256)]), quantize(256, [(0, 128), (128, 128)])]
         h_parts.append((512, 64, keep.tile([P, 64, PACK], BF16, name="h_bf512", tag="h_bf0", align_bytes=64)))
         on_gpsimd(512, plain)
         on_vector(576, 128)
@@ -207,14 +218,10 @@ def tile_picked_embpos_none_p_kernel(tc, x_words, x_scales, w1, w2_words, w2_sca
         finish(256, [(pairs[1], scalar)])
         on_vector(704, 64)
         on_vector(768, 128)
-        third = [quantize(576, 128), quantize(704, 64), quantize(512, 64)]
-        finish(512, [(third[2], scalar), (third[0], scalar), (third[1], scalar)])
+        third = quantize(512, [(64, 128), (192, 64), (0, 64)])
+        fourth = quantize(768, [(0, 128)])
+        finish(512, [(third, scalar)])
+        h_parts.append((896, 128, keep.tile([P, 128, PACK], BF16, name="h_bf896", tag="h_bf0", align_bytes=64)))
         on_vector(896, 128)
-        for first in (768, 896):
-            moving = quantize(first, 128)
-            result = keep.tile([P, N // P, 128], F32, name=f"result{first}")
-            for a, copy in enumerate((scalar, vector)):
-                bank = out_psum.tile([P, 128], F32, name="out_bank")
-                lone_pass(nc, bank[:], w2_tiles[a], moving)
-                copy(out=result[:, a, :], in_=bank[:])
-            nc.sync.dma_start(out=out_rows[:, :, first : first + 128], in_=result[:])
+        finish_shared(768, fourth)
+        finish_shared(896, quantize(896, [(0, 128)]))

@@ -177,51 +177,43 @@ def tile_picked_embpos_none_p_kernel(tc, x_words, x_scales, w1, w2_words, w2_sca
                 )
             return h_codes[:], h_plane[:]
 
-        out_rows = out.rearrange("(a p) s -> p a s", p=P)
         w2_tiles = [(w2_codes[:, a * P : (a + 1) * P], w2_plane[:, a * P : (a + 1) * P]) for a in range(N // P)]
-
-        def finish(first, runs):
-            total = sum(moving[0].shape[1] for moving, copy in runs)
-            result = keep.tile([P, N // P, total], F32, name=f"result{first}")
-            lo = 0
-            for moving, copy in runs:
-                width = moving[0].shape[1]
-                bank = out_psum.tile([P, N // P, width], F32, name="out_bank")
-                for a, stationary in enumerate(w2_tiles):
-                    lone_pass(nc, bank[:, a, :], stationary, moving)
-                copy(out=result[:, :, lo : lo + width], in_=bank[:])
-                lo += width
-            nc.sync.dma_start(out=out_rows[:, :, first : first + total], in_=result[:])
-
         scalar, vector = nc.scalar.copy, nc.vector.tensor_copy
 
-        def finish_shared(first, moving):
-            width = moving[0].shape[1]
-            result = keep.tile([P, N // P, width], F32, name=f"result{first}")
-            for a, copy in enumerate((scalar, vector)):
-                bank = out_psum.tile([P, width], F32, name="out_bank")
-                lone_pass(nc, bank[:], w2_tiles[a], moving)
-                copy(out=result[:, a, :], in_=bank[:])
-            nc.sync.dma_start(out=out_rows[:, :, first : first + width], in_=result[:])
+        def second(dst, tiles, moving, copy):
+            bank = out_psum.tile([P, len(tiles), moving[0].shape[1]], F32, name="out_bank")
+            for i, a in enumerate(tiles):
+                lone_pass(nc, bank[:, i, :], w2_tiles[a], moving)
+            copy(out=dst, in_=bank[:])
 
-        for first, count in ((0, 256), (256, 128), (384, 128), (576, 192), (768, 128)):
+        out_rows = out.rearrange("(a p) s -> p a s", p=P)
+
+        def result_tile(first, tiles, width):
+            return keep.tile([P, tiles, width], F32, name=f"result{first}_{tiles}")
+
+        for first, count in ((0, 256), (256, 128), (384, 128), (576, 192), (768, 256)):
             h_tile(first, count)
         on_gpsimd(384, out_of_psum(384, product(384, 128)))
         for first in (0, 128, 256):
             on_vector(first, 128)
         plain = out_of_psum(512, product(512, 64, out_psum, "out_bank"))
-        pairs = [quantize(0, [(0, 256)]), quantize(256, [(0, 128), (128, 128)])]
+        half = quantize(0, [(0, 256), (256, 128), (384, 128)])
         h_parts.append((512, 64, keep.tile([P, 64, PACK], BF16, name="h_bf512", tag="h_bf0", align_bytes=64)))
         on_gpsimd(512, plain)
         on_vector(576, 128)
-        finish(0, [(pairs[0], scalar)])
-        finish(256, [(pairs[1], scalar)])
+        for a in range(N // P):
+            result = keep.tile([P, 1, 512], F32, name=f"result_half{a}")
+            second(result[:], [a], half, scalar)
+            nc.sync.dma_start(out=out_rows[:, a : a + 1, :512], in_=result[:])
         on_vector(704, 64)
+        third = quantize(512, [(64, 128), (0, 64), (192, 64)])
         on_vector(768, 128)
-        third = quantize(512, [(64, 128), (192, 64), (0, 64)])
-        fourth = quantize(768, [(0, 128)])
-        finish(512, [(third, scalar)])
-        h_parts.append((896, 128, keep.tile([P, 128, PACK], BF16, name="h_bf896", tag="h_bf0", align_bytes=64)))
+        result = result_tile(512, 2, 256)
+        second(result[:], [0, 1], third, scalar)
+        nc.sync.dma_start(out=out_rows[:, :, 512:768], in_=result[:])
         on_vector(896, 128)
-        finish_shared(768, fourth)
-        finish_shared(896, quantize(896, [(0, 128)]))
+        result = result_tile(768, 2, 256)
+        for lo, moving in [(lo, quantize(768 + lo, [(0, 128)])) for lo in (0, 128)]:
+            for a, copy in enumerate((scalar, vector)):
+                second(result[:, a : a + 1, lo : lo + 128], [a], moving, copy)
+        nc.sync.dma_start(out=out_rows[:, :, 768:], in_=result[:])

@@ -75,7 +75,7 @@ def tile_picked_embpos_none_p_kernel(tc, x_words, x_scales, w1, w2_words, w2_sca
 
         pos_rows = pos.rearrange("(p t) s -> p t s", t=PACK)
         pos_parts = []
-        for load, (first, count) in enumerate(((0, 512), (512, 256), (768, 256))):
+        for load, (first, count) in enumerate(((0, 512), (512, 320), (832, 192))):
             part = keep.tile([P, PACK, count], F32, name=f"pos{load}")
             nc.sync.dma_start(out=part[:], in_=pos_rows[:, :, first : first + count])
             pos_parts.append((first, count, part))
@@ -191,7 +191,7 @@ def tile_picked_embpos_none_p_kernel(tc, x_words, x_scales, w1, w2_words, w2_sca
         def result_tile(first, tiles, width):
             return keep.tile([P, tiles, width], F32, name=f"result{first}_{tiles}")
 
-        for first, count in ((0, 256), (256, 128), (384, 128), (576, 192), (768, 256)):
+        for first, count in ((0, 256), (256, 128), (384, 128), (576, 256), (832, 192)):
             h_tile(first, count)
         on_gpsimd(384, out_of_psum(384, product(384, 128)))
         for first in (0, 128, 256):
@@ -205,15 +205,16 @@ def tile_picked_embpos_none_p_kernel(tc, x_words, x_scales, w1, w2_words, w2_sca
             result = keep.tile([P, 1, 512], F32, name=f"result_half{a}")
             second(result[:], [a], half, scalar)
             nc.sync.dma_start(out=out_rows[:, a : a + 1, :512], in_=result[:])
-        on_vector(704, 64)
-        third = quantize(512, [(64, 128), (0, 64), (192, 64)])
-        on_vector(768, 128)
-        result = result_tile(512, 2, 256)
-        second(result[:], [0, 1], third, scalar)
-        nc.sync.dma_start(out=out_rows[:, :, 512:768], in_=result[:])
-        on_vector(896, 128)
-        result = result_tile(768, 2, 256)
-        for lo, moving in [(lo, quantize(768 + lo, [(0, 128)])) for lo in (0, 128)]:
+        on_vector(704, 128)
+        runs = [(lo, quantize(512 + lo, [(0, width)])) for lo, width in ((64, 128), (0, 64), (192, 128))]
+        on_vector(832, 128)
+        result = result_tile(512, 2, 320)
+        for lo, moving in runs:
+            second(result[:, :, lo : lo + moving[0].shape[1]], [0, 1], moving, scalar)
+        nc.sync.dma_start(out=out_rows[:, :, 512:832], in_=result[:])
+        on_vector(960, 64)
+        result = result_tile(832, 2, 192)
+        for lo, moving in [(lo, quantize(832 + lo, [(0, width)])) for lo, width in ((0, 128), (128, 64))]:
             for a, copy in enumerate((scalar, vector)):
-                second(result[:, a : a + 1, lo : lo + 128], [a], moving, copy)
-        nc.sync.dma_start(out=out_rows[:, :, 768:], in_=result[:])
+                second(result[:, a : a + 1, lo : lo + moving[0].shape[1]], [a], moving, copy)
+        nc.sync.dma_start(out=out_rows[:, :, 832:], in_=result[:])

@@ -203,7 +203,8 @@ def tile_picked_embpos_none_p_kernel(tc, x_words, x_scales, w1, w2_words, w2_sca
         on_vector(576, 128)
         for a in range(N // P):
             result = keep.tile([P, 1, 512], F32, name=f"result_half{a}")
-            second(result[:], [a], half, scalar)
+            for lo in (0, 256):
+                second(result[:, :, lo : lo + 256], [a], (half[0][:, lo : lo + 256], half[1][:, lo : lo + 256]), scalar)
             nc.sync.dma_start(out=out_rows[:, a : a + 1, :512], in_=result[:])
         on_vector(704, 128)
         runs = [(lo, quantize(512 + lo, [(0, width)])) for lo, width in ((64, 128), (0, 64), (192, 128))]

@@ -180,8 +180,8 @@ def tile_picked_embpos_none_p_kernel(tc, x_words, x_scales, w1, w2_words, w2_sca
         w2_tiles = [(w2_codes[:, a * P : (a + 1) * P], w2_plane[:, a * P : (a + 1) * P]) for a in range(N // P)]
         scalar, vector = nc.scalar.copy, nc.vector.tensor_copy
 
-        def second(dst, tiles, moving, copy):
-            bank = out_psum.tile([P, len(tiles), moving[0].shape[1]], F32, name="out_bank")
+        def second(dst, tiles, moving, copy, pool=out_psum, name="out_bank"):
+            bank = pool.tile([P, len(tiles), moving[0].shape[1]], F32, name=name)
             for i, a in enumerate(tiles):
                 lone_pass(nc, bank[:, i, :], w2_tiles[a], moving)
             copy(out=dst, in_=bank[:])
@@ -217,5 +217,5 @@ def tile_picked_embpos_none_p_kernel(tc, x_words, x_scales, w1, w2_words, w2_sca
         result = result_tile(832, 2, 192)
         for lo, moving in [(lo, quantize(832 + lo, [(0, width)])) for lo, width in ((0, 128), (128, 64))]:
             for a, copy in enumerate((scalar, vector)):
-                second(result[:, a : a + 1, lo : lo + moving[0].shape[1]], [a], moving, copy)
+                second(result[:, a : a + 1, lo : lo + moving[0].shape[1]], [a], moving, copy, hid_psum, "hid_bank")
         nc.sync.dma_start(out=out_rows[:, :, 832:], in_=result[:])

@@ -111,7 +111,7 @@ def tile_picked_embpos_none_p_kernel(tc, x_words, x_scales, w1, w2_words, w2_sca
             )
 
         x_parts = []
-        for g, (first, count) in enumerate(((256, 256), (0, 256), (512, 512))):
+        for g, (first, count) in enumerate(((384, 128), (0, 384), (512, 512))):
             codes = keep.tile([P, count], U32, name=f"x_codes{g}", tag=f"shared{g}", align_bytes=64)
             entries = offsets[:, first // LIST_ROWS : (first + count) // LIST_ROWS]
             nc.vector.tensor_copy(out=codes[:], in_=table_codes[:].bitcast(U32).indirect(entries))

@@ -15,6 +15,7 @@ FP8X4 = mybir.dt.float8_e4m3fn_x4
 ADD = mybir.AluOpType.add
 
 P = 128
+AXI = 256
 PACK = 4
 LIST_ROWS = 16
 CHUNK = 128
@@ -54,29 +55,29 @@ def tile_picked_embpos_none_p_kernel(tc, x_words, x_scales, w1, w2_words, w2_sca
         out_psum = ctx.enter_context(tc.psum_pool(name="out_psum", bufs=4))
 
         offsets = keep.tile([P, S // LIST_ROWS], U16, name="offsets")
-        table_plane = keep.tile([P, T], U8, name="table_plane", align_bytes=64)
+        table_plane = keep.tile([P, T], U8, name="table_plane", align_bytes=AXI)
         nc.vector.memset(table_plane[:].bitcast(I32), 0)
 
         w1_rows = w1.rearrange("(p j) c -> p j c", j=PACK)
         w1_raw = []
         for half in range(2):
-            raw = keep.tile([P, 2, H], F32, name=f"w1_raw{half}")
+            raw = keep.tile([P, 2, H], F32, name=f"w1_raw{half}", align_bytes=AXI)
             nc.sync.dma_start(out=raw[:], in_=w1_rows[:, 2 * half : 2 * half + 2, :])
             w1_raw.append(raw)
             if half == 0:
                 nc.sync.dma_start(offsets[:], offs)
                 load_plane(nc, table_plane, x_scales[0])
-        table_codes = keep.tile([P, T], I32, name="table_codes", align_bytes=64)
+        table_codes = keep.tile([P, T], I32, name="table_codes", align_bytes=AXI)
         load_codes(nc, table_codes, x_words[0])
 
-        w2_codes = keep.tile([P, N], I32, name="w2_codes", align_bytes=64)
-        w2_plane = keep.tile([P, N], U8, name="w2_plane", align_bytes=64)
+        w2_codes = keep.tile([P, N], I32, name="w2_codes", align_bytes=AXI)
+        w2_plane = keep.tile([P, N], U8, name="w2_plane", align_bytes=AXI)
         nc.gpsimd.memset(w2_plane[:].bitcast(I32), 0)
 
         pos_rows = pos.rearrange("(p t) s -> p t s", t=PACK)
         pos_parts = []
         for load, (first, count) in enumerate(((0, 512), (512, 320), (832, 192))):
-            part = keep.tile([P, PACK, count], F32, name=f"pos{load}")
+            part = keep.tile([P, PACK, count], F32, name=f"pos{load}", align_bytes=AXI)
             nc.sync.dma_start(out=part[:], in_=pos_rows[:, :, first : first + count])
             pos_parts.append((first, count, part))
             if load == 1:
@@ -189,7 +190,7 @@ def tile_picked_embpos_none_p_kernel(tc, x_words, x_scales, w1, w2_words, w2_sca
         out_rows = out.rearrange("(a p) s -> p a s", p=P)
 
         def result_tile(first, tiles, width):
-            return keep.tile([P, tiles, width], F32, name=f"result{first}_{tiles}")
+            return keep.tile([P, tiles, width], F32, name=f"result{first}_{tiles}", align_bytes=AXI)
 
         for first, count in ((0, 256), (256, 128), (384, 128), (576, 256), (832, 192)):
             h_tile(first, count)
@@ -202,7 +203,7 @@ def tile_picked_embpos_none_p_kernel(tc, x_words, x_scales, w1, w2_words, w2_sca
         on_gpsimd(512, plain)
         on_vector(576, 128)
         for a in range(N // P):
-            result = keep.tile([P, 1, 512], F32, name=f"result_half{a}")
+            result = keep.tile([P, 1, 512], F32, name=f"result_half{a}", align_bytes=AXI)
             for lo in (0, 256):
                 second(result[:, :, lo : lo + 256], [a], (half[0][:, lo : lo + 256], half[1][:, lo : lo + 256]), scalar)
             nc.sync.dma_start(out=out_rows[:, a : a + 1, :512], in_=result[:])

from contextlib import ExitStack

import concourse.mybir as mybir

K, T, S, H, N = 512, 2048, 1024, 512, 256
FLOPS = 2 * K * H * S + 2 * H * N * S

F32 = mybir.dt.float32
BF16 = mybir.dt.bfloat16
I32 = mybir.dt.int32
U32 = mybir.dt.uint32
U16 = mybir.dt.uint16
U8 = mybir.dt.uint8
FP8X4 = mybir.dt.float8_e4m3fn_x4
ADD = mybir.AluOpType.add

P = 128
AXI = 256
PACK = 4
LIST_ROWS = 16
CHUNK = 128
PAIR = 2 * CHUNK
GATHER = 512


def load_plane(nc, plane, rows):
    for q in range(4):
        nc.sync.dma_start(
            out=plane[32 * q : 32 * q + 4, :].bitcast(I32),
            in_=rows[4 * q : 4 * q + 4, :].bitcast(I32),
        )


def load_codes(nc, codes, words):
    nc.sync.dma_start(out=codes[:], in_=words.rearrange("p c j -> p (c j)").bitcast(I32))


def lone_pass(nc, dst, stationary, moving):
    nc.tensor.matmul_mx(
        out=dst,
        lhsT=stationary[0].bitcast(FP8X4),
        lhsT_scale=stationary[1],
        rhs=moving[0].bitcast(FP8X4),
        rhs_scale=moving[1],
        start=True,
        stop=True,
    )


def tile_picked_embpos_none_p_kernel(tc, x_words, x_scales, w1, w2_words, w2_scales, pos, offs, out):
    nc = tc.nc
    with ExitStack() as ctx:
        keep = ctx.enter_context(tc.tile_pool(name="keep", bufs=1))
        hid_psum = ctx.enter_context(tc.psum_pool(name="hid_psum", bufs=4))
        out_psum = ctx.enter_context(tc.psum_pool(name="out_psum", bufs=4))

        offsets = keep.tile([P, S // LIST_ROWS], U16, name="offsets")
        table_plane = keep.tile([P, T], U8, name="table_plane", align_bytes=AXI)
        nc.vector.memset(table_plane[:].bitcast(I32), 0)

        w1_rows = w1.rearrange("(p j) c -> p j c", j=PACK)
        w1_raw = []
        for half in range(2):
            raw = keep.tile([P, 2, H], F32, name=f"w1_raw{half}", align_bytes=AXI)
            nc.sync.dma_start(out=raw[:], in_=w1_rows[:, 2 * half : 2 * half + 2, :])
            w1_raw.append(raw)
            if half == 0:
                nc.sync.dma_start(offsets[:], offs)
                load_plane(nc, table_plane, x_scales[0])
        table_codes = keep.tile([P, T], I32, name="table_codes", align_bytes=AXI)
        load_codes(nc, table_codes, x_words[0])

        w2_codes = keep.tile([P, N], I32, name="w2_codes", align_bytes=AXI)
        w2_plane = keep.tile([P, N], U8, name="w2_plane", align_bytes=AXI)
        nc.gpsimd.memset(w2_plane[:].bitcast(I32), 0)

        pos_rows = pos.rearrange("(p t) s -> p t s", t=PACK)
        pos_parts = []
        for load, (first, count) in enumerate(((0, 512), (512, 320), (832, 192))):
            part = keep.tile([P, PACK, count], F32, name=f"pos{load}", align_bytes=AXI)
            nc.sync.dma_start(out=part[:], in_=pos_rows[:, :, first : first + count])
            pos_parts.append((first, count, part))
            if load == 1:
                load_codes(nc, w2_codes, w2_words[0])
                load_plane(nc, w2_plane, w2_scales[0])

        x_plane = keep.tile([P, S], U8, name="x_plane", align_bytes=64)
        nc.vector.tensor_copy(out=x_plane[:], in_=table_plane[:].indirect(offsets[:]))

        w1_codes = keep.tile([P, H], U32, name="w1_codes", align_bytes=64)
        w1_plane = keep.tile([P, H], U8, name="w1_plane", align_bytes=64)
        w1_grouped = [
            keep.tile([P, 2, P, PACK], BF16, name=f"w1_grouped{u}", tag=f"shared{u}", align_bytes=64) for u in range(2)
        ]
        def deal_w1(copy, half, u, m0, m1):
            copy(
                out=w1_grouped[u][:, :, m0:m1, 2 * half : 2 * half + 2].rearrange("p t m j -> p m j t"),
                in_=w1_raw[half][:].rearrange("p j (m t) -> p m j t", t=PACK)[:, m0:m1, :, 2 * u : 2 * u + 2],
            )

        deal_w1(nc.scalar.copy, 0, 0, 0, P)
        deal_w1(nc.vector.tensor_copy, 0, 1, 0, P)
        deal_w1(nc.scalar.copy, 1, 0, 0, P)
        deal_w1(nc.scalar.copy, 1, 1, 0, P // 2)
        deal_w1(nc.vector.tensor_copy, 1, 1, P // 2, P)
        for u in range(2):
            cols = slice(u * 2 * P, (u + 1) * 2 * P)
            nc.vector.quantize_mx(
                out=w1_codes[:, cols].bitcast(FP8X4),
                scales=w1_plane[:, cols],
                in_=w1_grouped[u][:].rearrange("p t m j -> p (t m j)"),
            )

        x_parts = []
        for g, (first, count) in enumerate(((384, 128), (0, 384), (512, 512))):
            codes = keep.tile([P, count], U32, name=f"x_codes{g}", tag=f"shared{g}", align_bytes=64)
            entries = offsets[:, first // LIST_ROWS : (first + count) // LIST_ROWS]
            nc.vector.tensor_copy(out=codes[:], in_=table_codes[:].bitcast(U32).indirect(entries))
            x_parts.append((first, count, codes))

        def holder(parts, first):
            return [(tile, first - lo) for lo, count, tile in parts if lo <= first < lo + count][0]

        def product(first, width, pool=hid_psum, name="hid_bank"):
            codes, lo = holder(x_parts, first)
            picked = (codes[:, lo : lo + width], x_plane[:, first : first + width])
            bank = pool.tile([P, PACK, width], F32, name=name)
            for t in range(PACK):
                cols = slice(t * P, (t + 1) * P)
                lone_pass(nc, bank[:, t, :], (w1_codes[:, cols], w1_plane[:, cols]), picked)
            return bank

        h_parts = []

        def h_tile(first, count):
            h_parts.append((first, count, keep.tile([P, count, PACK], BF16, name=f"h_bf{first}", tag=f"h_bf{first}", align_bytes=64)))

        def add_pos(engine, first, summand):
            width = summand.shape[2]
            part, lo = holder(pos_parts, first)
            h_bf, at = holder(h_parts, first)
            engine.tensor_tensor(
                out=h_bf[:, at : at + width, :].rearrange("p (d e) t -> p d t e", e=2),
                in0=summand[:].rearrange("p t (d e) -> p d t e", e=2),
                in1=part[:, :, lo : lo + width].rearrange("p t (d e) -> p d t e", e=2),
                op=ADD,
            )

        def on_vector(first, width):
            add_pos(nc.vector, first, product(first, width))

        def out_of_psum(first, bank):
            plain = keep.tile([P, bank.shape[2] // 4, PACK, 4], F32, name=f"plain{first}")
            nc.scalar.copy(out=plain[:], in_=bank[:].rearrange("p t (d e) -> p d t e", e=4))
            return plain

        def on_gpsimd(first, plain):
            width = 4 * plain.shape[1]
            part, lo = holder(pos_parts, first)
            h_bf, at = holder(h_parts, first)
            nc.gpsimd.tensor_tensor(
                out=h_bf[:, at : at + width, :].rearrange("p (d e) t -> p d t e", e=4),
                in0=plain[:],
                in1=part[:, :, lo : lo + width].rearrange("p t (d e) -> p d t e", e=4),
                op=ADD,
            )

        def quantize(first, runs):
            total = sum(width for lo, width in runs)
            h_codes = keep.tile([P, total], U32, name=f"h_codes{first}", align_bytes=64)
            h_plane = keep.tile([P, total], U8, name=f"h_plane{first}", align_bytes=64)
            for lo, width in runs:
                h_bf, at = holder(h_parts, first + lo)
                nc.vector.quantize_mx(
                    out=h_codes[:, lo : lo + width].bitcast(FP8X4),
                    scales=h_plane[:, lo : lo + width],
                    in_=h_bf[:, at : at + width, :].rearrange("p s t -> p (s t)"),
                )
            return h_codes[:], h_plane[:]

        w2_tiles = [(w2_codes[:, a * P : (a + 1) * P], w2_plane[:, a * P : (a + 1) * P]) for a in range(N // P)]
        scalar, vector = nc.scalar.copy, nc.vector.tensor_copy

        def second(dst, tiles, moving, copy, pool=out_psum, name="out_bank"):
            bank = pool.tile([P, len(tiles), moving[0].shape[1]], F32, name=name)
            for i, a in enumerate(tiles):
                lone_pass(nc, bank[:, i, :], w2_tiles[a], moving)
            copy(out=dst, in_=bank[:])

        out_rows = out.rearrange("(a p) s -> p a s", p=P)

        def result_tile(first, tiles, width):
            return keep.tile([P, tiles, width], F32, name=f"result{first}_{tiles}", align_bytes=AXI)

        for first, count in ((0, 256), (256, 128), (384, 128), (576, 256), (832, 192)):
            h_tile(first, count)
        on_gpsimd(384, out_of_psum(384, product(384, 128)))
        for first in (0, 128, 256):
            on_vector(first, 128)
        plain = out_of_psum(512, product(512, 64, out_psum, "out_bank"))
        half = quantize(0, [(0, 256), (256, 128), (384, 128)])
        h_parts.append((512, 64, keep.tile([P, 64, PACK], BF16, name="h_bf512", tag="h_bf0", align_bytes=64)))
        on_gpsimd(512, plain)
        on_vector(576, 128)
        for a in range(N // P):
            result = keep.tile([P, 1, 512], F32, name=f"result_half{a}", align_bytes=AXI)
            for lo in (0, 256):
                second(result[:, :, lo : lo + 256], [a], (half[0][:, lo : lo + 256], half[1][:, lo : lo + 256]), scalar)
            nc.sync.dma_start(out=out_rows[:, a : a + 1, :512], in_=result[:])
        on_vector(704, 128)
        runs = [(lo, quantize(512 + lo, [(0, width)])) for lo, width in ((64, 128), (0, 64), (192, 128))]
        on_vector(832, 128)
        result = result_tile(512, 2, 320)
        for lo, moving in runs:
            second(result[:, :, lo : lo + moving[0].shape[1]], [0, 1], moving, scalar)
        nc.sync.dma_start(out=out_rows[:, :, 512:832], in_=result[:])
        on_vector(960, 64)
        result = result_tile(832, 2, 192)
        for lo, moving in [(lo, quantize(832 + lo, [(0, width)])) for lo, width in ((0, 128), (128, 64))]:
            for a, copy in enumerate((scalar, vector)):
                second(result[:, a : a + 1, lo : lo + moving[0].shape[1]], [a], moving, copy, hid_psum, "hid_bank")
        nc.sync.dma_start(out=out_rows[:, :, 832:], in_=result[:])
